import numpy as np
import ml_dtypes


def mxq(x, axis, fmt="e4m3"):
    dtype, down = {"e4m3": (ml_dtypes.float8_e4m3fn, 7), "e5m2": (ml_dtypes.float8_e5m2, 14)}[fmt]
    v = np.moveaxis(np.asarray(x, np.float32).astype(ml_dtypes.bfloat16).astype(np.float64), axis, -1)
    blocks = v.reshape(v.shape[:-1] + (-1, 32))
    amax = np.abs(blocks).max(-1, keepdims=True)
    byte = np.maximum(np.where(amax > 0, np.frexp(amax)[1] - 1 + 127, 0) - down, 1)
    scale = np.exp2(byte - 127.0)
    codes = (blocks / scale).astype(np.float32).astype(dtype).astype(np.float64)
    return np.moveaxis((codes * scale).reshape(v.shape), -1, axis)


WIDE = False


def mx_kscale(k):
    if not WIDE:
        return np.ones(k)
    levels = np.array([10, -10, 5, -5, 0])
    if k % 512:
        return np.exp2(np.random.permutation(np.resize(levels, k // 32))).repeat(32)
    a = np.empty((k // 512, 16))
    for p in range(k // 512):
        a[p, :8] = np.random.permutation(np.resize(levels, 8))
        for g in range(8):
            far = levels[np.abs(levels - a[p, g]) >= 10]
            a[p, g + 8] = far[np.random.randint(len(far))]
    return np.exp2(a.ravel()).repeat(32)


def f64(x):
    return np.asarray(x).astype(np.float64)


def striped(idx):
    return np.tile(idx.reshape(-1, 16).T, (8, 1)).astype(np.uint16)


def unstriped(offs):
    return offs[:16].T.reshape(-1).astype(np.int64)


def pack_weight(w):
    k, n = w.shape
    w = f64(np.asarray(w, np.float32).astype(ml_dtypes.bfloat16)).reshape(k // 32, 32, n)
    amax = np.abs(w).max(1)
    byte = np.clip(np.where(amax > 0, np.frexp(amax)[1] - 1 + 127 - 7, 1), 1, 254)
    scaled = (w * np.exp2(127.0 - byte)[:, None, :]).reshape(k, n).astype(np.float32)
    words = np.ascontiguousarray(scaled.reshape(k // 512, 128, 4, n).transpose(0, 1, 3, 2)).astype(ml_dtypes.float8_e4m3fn).view(np.uint8)
    return words, np.ascontiguousarray(byte.astype(np.uint8).reshape(k // 512, 16, n))


def unpack_weight(words, scales):
    g, p, n, _ = words.shape
    vals = np.ascontiguousarray(words).view(ml_dtypes.float8_e4m3fn).astype(np.float64) * np.repeat(np.exp2(scales.astype(np.float64) - 127.0), 8, axis=1)[..., None]
    return vals.transpose(0, 1, 3, 2).reshape(g * 512, n)


def relu(v):
    return np.maximum(v, 0.0)


K, T, S, H, N = 1024, 2048, 512, 512, 128


def setup_inputs():
    n = np.random.standard_normal
    s = mx_kscale(K)[:, None]
    u = mx_kscale(H)
    packed_w2 = pack_weight(n((H, N)) / np.sqrt(H) / u[:, None])
    return {
        "xT": (n((K, T)) * s).astype(np.float32),
        "w1": (n((K, H)) / np.sqrt(K) / s).astype(np.float32),
        "w2_words": packed_w2[0],
        "w2_scales": packed_w2[1],
        "gamma": (np.random.uniform(0.5, 1.5, (H, 1)) * u[:, None]).astype(np.float32),
        "offs": striped(np.random.permutation(T)[:S]),
    }


def reference(xT, w1, w2_words, w2_scales, gamma, offs):
    xq = mxq(f64(xT)[:, unstriped(offs)], 0, "e4m3")
    h = mxq(f64(w1), 0, "e4m3").T @ xq
    hn = (h - h.mean(axis=1, keepdims=True)) / np.sqrt(h.var(axis=1, keepdims=True) + 1e-5)
    z = relu(f64(gamma) * hn)
    return unpack_weight(w2_words, w2_scales).T @ mxq(z, 0, "e4m3")

@@ -1,0 +1,167 @@
+from contextlib import ExitStack
+
+import concourse.mybir as mybir
+
+K, T, S, H, N = 1024, 2048, 512, 512, 128
+FLOPS = 2 * K * H * S + 2 * H * N * S
+EPS = 1e-5
+
+F32 = mybir.dt.float32
+BF16 = mybir.dt.bfloat16
+I32 = mybir.dt.int32
+U32 = mybir.dt.uint32
+U16 = mybir.dt.uint16
+U8 = mybir.dt.uint8
+FP8X4 = mybir.dt.float8_e4m3fn_x4
+ALU = mybir.AluOpType
+ACT = mybir.ActivationFunctionType
+
+P = 128
+PACK = 4
+K_PASS = P * PACK
+PASSES = K // K_PASS
+HALF = S // 2
+M_VECTOR = 88
+
+
+def tile_picked_inorm_relu_e_kernel(tc, xT, w1, w2_words, w2_scales, gamma, offs, out):
+    nc = tc.nc
+    with ExitStack() as ctx:
+        keep = ctx.enter_context(tc.tile_pool(name="keep", bufs=1))
+        psum = ctx.enter_context(tc.psum_pool(name="psum", bufs=1))
+
+        offsets = keep.tile([P, S // 16], U16, name="offsets")
+        x_rows = xT.rearrange("(g p j) c -> g j p c", p=P, j=PACK)
+        planes = {}
+        for g in range(PASSES):
+            for j in range(PACK):
+                planes[g, j] = keep.tile([P, T], F32, name=f"plane{g}{j}")
+                nc.sync.dma_start(planes[g, j][:], x_rows[g, j])
+                if (g, j) == (0, 0):
+                    nc.sync.dma_start(offsets[:], offs)
+        w_raw = []
+        for g in range(PASSES):
+            raw = keep.tile([P, PACK, H], F32, name=f"w_raw{g}")
+            nc.sync.dma_start(raw[:], w1[g * K_PASS : (g + 1) * K_PASS, :].rearrange("(p j) c -> p j c", j=PACK))
+            w_raw.append(raw)
+
+        w2_scale = keep.tile([P, N], U8, name="w2_scale", align_bytes=64)
+        w2_code = keep.tile([P, N], U32, name="w2_code", align_bytes=64)
+        gamma_sb = keep.tile([P, PACK], F32, name="gamma_sb")
+        nc.gpsimd.memset(w2_scale[:], 0)
+        nc.gpsimd.dma_start(gamma_sb[:], gamma.rearrange("(p t) o -> p (t o)", t=PACK))
+        nc.gpsimd.dma_start(w2_code[:].bitcast(I32), w2_words[0].rearrange("p n t -> p (n t)").bitcast(I32))
+        for q in range(4):
+            nc.gpsimd.dma_start(
+                w2_scale[32 * q : 32 * q + 4, :].bitcast(I32), w2_scales[0, 4 * q : 4 * q + 4, :].bitcast(I32)
+            )
+
+        warm_in = keep.tile([P, 1], F32, name="warm_in")
+        warm_out = keep.tile([P, 1], F32, name="warm_out")
+        nc.vector.memset(warm_in[:], 1.0)
+        nc.scalar.activation(warm_out[:], warm_in[:], ACT.Abs_reciprocal_sqrt)
+        neg_gamma = keep.tile([P, PACK], F32, name="neg_gamma")
+        factors = keep.tile([P, PACK, 2], F32, name="factors")
+        nc.scalar.activation(neg_gamma[:], gamma_sb[:], ACT.Copy, scale=-1.0)
+        nc.scalar.activation(factors[:, :, 0], gamma_sb[:], ACT.Copy)
+
+        x_code, x_scale = [], []
+        for g in range(PASSES):
+            picked = keep.tile([P, S, PACK], BF16, name=f"picked{g}", align_bytes=64)
+            for j in range(PACK):
+                nc.vector.tensor_copy(picked[:, :, j], planes[g, j][:].indirect(offsets[:]))
+            code = keep.tile([P, S], U32, name=f"x_code{g}", align_bytes=64)
+            scale = keep.tile([P, S], U8, name=f"x_scale{g}", align_bytes=64)
+            nc.vector.quantize_mx(code[:].bitcast(FP8X4), scale[:], picked[:].rearrange("p s j -> p (s j)"))
+            x_code.append(code)
+            x_scale.append(scale)
+
+        pieces = [(t, 0, S) for t in range(PACK - 1)] + [(PACK - 1, 0, HALF), (PACK - 1, HALF, S)]
+        banks = {}
+        for t, lo, hi in pieces:
+            banks[t, lo] = psum.tile([P, hi - lo], F32, name=f"h{t}_{lo}")
+        for g in range(PASSES):
+            dealt = keep.tile([P, PACK, P, PACK], BF16, name=f"dealt{g}", align_bytes=64)
+            dst = dealt[:].rearrange("p t m j -> p m t j")
+            src = w_raw[g][:].rearrange("p j (m t) -> p m t j", t=PACK)
+            nc.vector.tensor_copy(dst[:, :M_VECTOR], src[:, :M_VECTOR])
+            nc.scalar.copy(dst[:, M_VECTOR:], src[:, M_VECTOR:])
+            for t in range(PACK):
+                code = keep.tile([P, P], U32, name=f"w_code{g}{t}", align_bytes=64)
+                scale = keep.tile([P, P], U8, name=f"w_scale{g}{t}", align_bytes=64)
+                nc.vector.quantize_mx(code[:].bitcast(FP8X4), scale[:], dealt[:, t].rearrange("p m j -> p (m j)"))
+                for tt, lo, hi in pieces:
+                    if tt == t:
+                        nc.tensor.matmul_mx(
+                            banks[t, lo][:],
+                            lhsT=code[:].bitcast(FP8X4),
+                            lhsT_scale=scale[:],
+                            rhs=x_code[g][:, lo:hi].bitcast(FP8X4),
+                            rhs_scale=x_scale[g][:, lo:hi],
+                            start=(g == 0),
+                            stop=(g == PASSES - 1),
+                        )
+
+        def h_cols(t, lo, hi):
+            if (t, HALF) in banks and lo >= HALF:
+                return banks[t, HALF][:, lo - HALF : hi - HALF]
+            return banks[t, 0][:, lo:hi]
+
+        stats = [keep.tile([P, 2, 6], F32, name=f"stats{t}") for t in range(PACK)]
+        moments = [keep.tile([P, 2], F32, name=f"moments{t}") for t in range(PACK)]
+        rstd = [keep.tile([P, 1], F32, name=f"rstd{t}") for t in range(PACK)]
+        affine = [keep.tile([P, 2], F32, name=f"affine{t}") for t in range(PACK)]
+        z_planes = [keep.tile([P, PACK, HALF], BF16, name=f"z_planes{u}") for u in range(2)]
+
+        def half_stats(t, u):
+            nc.vector.bn_stats(stats[t][:, u, :], h_cols(t, u * HALF, (u + 1) * HALF))
+
+        def finish_stats(t):
+            nc.vector.bn_aggr(moments[t][:], stats[t][:].rearrange("p u s -> p (u s)"))
+            nc.scalar.activation(rstd[t][:], moments[t][:, 1:2], ACT.Abs_reciprocal_sqrt, bias=EPS)
+            nc.scalar.activation(factors[:, t, 1:2], moments[t][:, 0:1], ACT.Copy, scale=neg_gamma[:, t : t + 1])
+            nc.scalar.activation(affine[t][:], factors[:, t, :], ACT.Copy, scale=rstd[t][:])
+
+        def normalise_scalar(t, u):
+            nc.scalar.activation(
+                z_planes[u][:, t, :], h_cols(t, u * HALF, (u + 1) * HALF), ACT.Relu,
+                scale=affine[t][:, 0:1], bias=affine[t][:, 1:2],
+            )
+
+        half_stats(0, 0)
+        half_stats(0, 1)
+        for t in range(1, PACK):
+            half_stats(t, 0)
+            finish_stats(t - 1)
+            half_stats(t, 1)
+            normalise_scalar(t - 1, 0)
+            normalise_scalar(t - 1, 1)
+        last = PACK - 1
+        finish_stats(last)
+        nc.vector.tensor_scalar(
+            z_planes[0][:, last, :], h_cols(last, 0, HALF), affine[last][:, 0:1], affine[last][:, 1:2], ALU.mult, ALU.add
+        )
+        normalise_scalar(last, 1)
+
+        for u in range(2):
+            woven = keep.tile([P, HALF, PACK], BF16, name=f"woven{u}", align_bytes=64)
+            src = z_planes[u][:].rearrange("p t s -> p s t")
+            if u == 0:
+                nc.vector.tensor_scalar_max(woven[:], src, 0.0)
+            else:
+                nc.vector.tensor_copy(woven[:, :P], src[:, :P])
+                nc.scalar.copy(woven[:, P:], src[:, P:])
+            code = keep.tile([P, HALF], U32, name=f"z_code{u}", align_bytes=64)
+            scale = keep.tile([P, HALF], U8, name=f"z_scale{u}", align_bytes=64)
+            nc.vector.quantize_mx(code[:].bitcast(FP8X4), scale[:], woven[:].rearrange("p s t -> p (s t)"))
+            acc = psum.tile([P, HALF], F32, name=f"acc{u}")
+            nc.tensor.matmul_mx(
+                acc[:], lhsT=w2_code[:].bitcast(FP8X4), lhsT_scale=w2_scale[:],
+                rhs=code[:].bitcast(FP8X4), rhs_scale=scale[:], start=True, stop=True,
+            )
+            result = keep.tile([P, HALF], F32, name=f"result{u}")
+            if u == 0:
+                nc.scalar.copy(result[:], acc[:])
+            else:
+                nc.vector.tensor_copy(result[:], acc[:])
+            nc.sync.dma_start(out[:, u * HALF : (u + 1) * HALF], result[:])

@@ -22,6 +22,8 @@ K_PASS = P * PACK
 PASSES = K // K_PASS
 HALF = S // 2
 M_VECTOR = 88
+M_VECTOR_LATE = 48
+X_LOADS = ((0, 0, 2), (0, 2, 2), (1, 0, 2), (1, 2, 1), (1, 3, 1))
 
 
 def tile_picked_inorm_relu_e_kernel(tc, xT, w1, w2_words, w2_scales, gamma, offs, out):
@@ -31,14 +33,17 @@ def tile_picked_inorm_relu_e_kernel(tc, xT, w1, w2_words, w2_scales, gamma, offs
         psum = ctx.enter_context(tc.psum_pool(name="psum", bufs=1))
 
         offsets = keep.tile([P, S // 16], U16, name="offsets")
-        x_rows = xT.rearrange("(g p j) c -> g j p c", p=P, j=PACK)
-        planes = {}
-        for g in range(PASSES):
-            for j in range(PACK):
-                planes[g, j] = keep.tile([P, T], F32, name=f"plane{g}{j}")
-                nc.sync.dma_start(planes[g, j][:], x_rows[g, j])
-                if (g, j) == (0, 0):
-                    nc.sync.dma_start(offsets[:], offs)
+        gamma_sb = keep.tile([P, PACK], F32, name="gamma_sb")
+        x_rows = xT.rearrange("(g p j) c -> g p j c", p=P, j=PACK)
+        windows = {}
+        for g, j0, count in X_LOADS:
+            rows = keep.tile([P, count, T], F32, name=f"x_rows{g}{j0}")
+            nc.sync.dma_start(rows[:], x_rows[g, :, j0 : j0 + count, :])
+            for j in range(count):
+                windows[g, j0 + j] = rows[:, j, :]
+            if (g, j0) == (0, 0):
+                nc.sync.dma_start(offsets[:], offs)
+                nc.sync.dma_start(gamma_sb[:], gamma.rearrange("(p t) o -> p (t o)", t=PACK))
         w_raw = []
         for g in range(PASSES):
             raw = keep.tile([P, PACK, H], F32, name=f"w_raw{g}")
@@ -47,12 +52,10 @@ def tile_picked_inorm_relu_e_kernel(tc, xT, w1, w2_words, w2_scales, gamma, offs
 
         w2_scale = keep.tile([P, N], U8, name="w2_scale", align_bytes=64)
         w2_code = keep.tile([P, N], U32, name="w2_code", align_bytes=64)
-        gamma_sb = keep.tile([P, PACK], F32, name="gamma_sb")
-        nc.gpsimd.memset(w2_scale[:], 0)
-        nc.gpsimd.dma_start(gamma_sb[:], gamma.rearrange("(p t) o -> p (t o)", t=PACK))
-        nc.gpsimd.dma_start(w2_code[:].bitcast(I32), w2_words[0].rearrange("p n t -> p (n t)").bitcast(I32))
+        nc.vector.memset(w2_scale[:].bitcast(I32), 0)
+        nc.sync.dma_start(w2_code[:].bitcast(I32), w2_words[0].rearrange("p n t -> p (n t)").bitcast(I32))
         for q in range(4):
-            nc.gpsimd.dma_start(
+            nc.sync.dma_start(
                 w2_scale[32 * q : 32 * q + 4, :].bitcast(I32), w2_scales[0, 4 * q : 4 * q + 4, :].bitcast(I32)
             )
 
@@ -67,12 +70,16 @@ def tile_picked_inorm_relu_e_kernel(tc, xT, w1, w2_words, w2_scales, gamma, offs
 
         x_code, x_scale = [], []
         for g in range(PASSES):
-            picked = keep.tile([P, S, PACK], BF16, name=f"picked{g}", align_bytes=64)
+            picked = [keep.tile([P, PACK, HALF], F32, name=f"picked{g}{u}") for u in range(2)]
             for j in range(PACK):
-                nc.vector.tensor_copy(picked[:, :, j], planes[g, j][:].indirect(offsets[:]))
+                for u in range(2):
+                    nc.vector.tensor_copy(picked[u][:, j, :], windows[g, j].indirect(offsets[:, 16 * u : 16 * (u + 1)]))
+            x_woven = keep.tile([P, S, PACK], BF16, name=f"x_woven{g}", align_bytes=64)
+            nc.scalar.copy(x_woven[:, :HALF], picked[0][:].rearrange("p j s -> p s j"))
+            nc.vector.tensor_copy(x_woven[:, HALF:], picked[1][:].rearrange("p j s -> p s j"))
             code = keep.tile([P, S], U32, name=f"x_code{g}", align_bytes=64)
             scale = keep.tile([P, S], U8, name=f"x_scale{g}", align_bytes=64)
-            nc.vector.quantize_mx(code[:].bitcast(FP8X4), scale[:], picked[:].rearrange("p s j -> p (s j)"))
+            nc.vector.quantize_mx(code[:].bitcast(FP8X4), scale[:], x_woven[:].rearrange("p s j -> p (s j)"))
             x_code.append(code)
             x_scale.append(scale)
 
@@ -81,26 +88,30 @@ def tile_picked_inorm_relu_e_kernel(tc, xT, w1, w2_words, w2_scales, gamma, offs
         for t, lo, hi in pieces:
             banks[t, lo] = psum.tile([P, hi - lo], F32, name=f"h{t}_{lo}")
         for g in range(PASSES):
-            dealt = keep.tile([P, PACK, P, PACK], BF16, name=f"dealt{g}", align_bytes=64)
-            dst = dealt[:].rearrange("p t m j -> p m t j")
             src = w_raw[g][:].rearrange("p j (m t) -> p m t j", t=PACK)
-            nc.vector.tensor_copy(dst[:, :M_VECTOR], src[:, :M_VECTOR])
-            nc.scalar.copy(dst[:, M_VECTOR:], src[:, M_VECTOR:])
-            for t in range(PACK):
-                code = keep.tile([P, P], U32, name=f"w_code{g}{t}", align_bytes=64)
-                scale = keep.tile([P, P], U8, name=f"w_scale{g}{t}", align_bytes=64)
-                nc.vector.quantize_mx(code[:].bitcast(FP8X4), scale[:], dealt[:, t].rearrange("p m j -> p (m j)"))
-                for tt, lo, hi in pieces:
-                    if tt == t:
-                        nc.tensor.matmul_mx(
-                            banks[t, lo][:],
-                            lhsT=code[:].bitcast(FP8X4),
-                            lhsT_scale=scale[:],
-                            rhs=x_code[g][:, lo:hi].bitcast(FP8X4),
-                            rhs_scale=x_scale[g][:, lo:hi],
-                            start=(g == 0),
-                            stop=(g == PASSES - 1),
-                        )
+            for t0 in (0, 2):
+                dealt = keep.tile([P, 2, P, PACK], BF16, name=f"dealt{g}{t0}", align_bytes=64)
+                dst = dealt[:].rearrange("p t m j -> p m t j")
+                split = M_VECTOR_LATE if (g, t0) == (PASSES - 1, 2) else M_VECTOR
+                nc.vector.tensor_copy(dst[:, :split], src[:, :split, t0 : t0 + 2])
+                nc.scalar.copy(dst[:, split:], src[:, split:, t0 : t0 + 2])
+                for t in (t0, t0 + 1):
+                    code = keep.tile([P, P], U32, name=f"w_code{g}{t}", align_bytes=64)
+                    scale = keep.tile([P, P], U8, name=f"w_scale{g}{t}", align_bytes=64)
+                    nc.vector.quantize_mx(
+                        code[:].bitcast(FP8X4), scale[:], dealt[:, t - t0].rearrange("p m j -> p (m j)")
+                    )
+                    for tt, lo, hi in pieces:
+                        if tt == t:
+                            nc.tensor.matmul_mx(
+                                banks[t, lo][:],
+                                lhsT=code[:].bitcast(FP8X4),
+                                lhsT_scale=scale[:],
+                                rhs=x_code[g][:, lo:hi].bitcast(FP8X4),
+                                rhs_scale=x_scale[g][:, lo:hi],
+                                start=(g == 0),
+                                stop=(g == PASSES - 1),
+                            )
 
         def h_cols(t, lo, hi):
             if (t, HALF) in banks and lo >= HALF:

@@ -21,9 +21,10 @@ PACK = 4
 K_PASS = P * PACK
 PASSES = K // K_PASS
 HALF = S // 2
-M_VECTOR = 88
-M_VECTOR_LATE = 48
-X_LOADS = ((0, 0, 2), (0, 2, 2), (1, 0, 2), (1, 2, 1), (1, 3, 1))
+QUARTER = S // 4
+W_SPLITS = {(0, 0): 0, (0, 2): 96, (1, 0): 56, (1, 2): 72}
+Z_SPLITS = (128, 128, 64, 0)
+X_PIECES = ((0, 128, False), (128, 256, False), (256, 384, True), (384, 512, True))
 
 
 def tile_picked_inorm_relu_e_kernel(tc, xT, w1, w2_words, w2_scales, gamma, offs, out):
@@ -34,21 +35,27 @@ def tile_picked_inorm_relu_e_kernel(tc, xT, w1, w2_words, w2_scales, gamma, offs
 
         offsets = keep.tile([P, S // 16], U16, name="offsets")
         gamma_sb = keep.tile([P, PACK], F32, name="gamma_sb")
-        x_rows = xT.rearrange("(g p j) c -> g p j c", p=P, j=PACK)
-        windows = {}
-        for g, j0, count in X_LOADS:
-            rows = keep.tile([P, count, T], F32, name=f"x_rows{g}{j0}")
-            nc.sync.dma_start(rows[:], x_rows[g, :, j0 : j0 + count, :])
-            for j in range(count):
-                windows[g, j0 + j] = rows[:, j, :]
-            if (g, j0) == (0, 0):
-                nc.sync.dma_start(offsets[:], offs)
-                nc.sync.dma_start(gamma_sb[:], gamma.rearrange("(p t) o -> p (t o)", t=PACK))
-        w_raw = []
-        for g in range(PASSES):
-            raw = keep.tile([P, PACK, H], F32, name=f"w_raw{g}")
-            nc.sync.dma_start(raw[:], w1[g * K_PASS : (g + 1) * K_PASS, :].rearrange("(p j) c -> p j c", j=PACK))
-            w_raw.append(raw)
+        x_rows = xT.rearrange("(g p j) c -> g j p c", p=P, j=PACK)
+        w_rows = w1.rearrange("(g p j) c -> g p j c", p=P, j=PACK)
+        planes = {}
+        w_raw = {}
+
+        def load_x(g, j):
+            planes[g, j] = keep.tile([P, T], F32, name=f"plane{g}{j}")
+            nc.sync.dma_start(planes[g, j][:], x_rows[g, j])
+
+        def load_w(g):
+            w_raw[g] = keep.tile([P, PACK, H], F32, name=f"w_raw{g}")
+            nc.sync.dma_start(w_raw[g][:], w_rows[g])
+
+        load_x(0, 0)
+        nc.sync.dma_start(offsets[:], offs)
+        nc.sync.dma_start(gamma_sb[:], gamma.rearrange("(p t) o -> p (t o)", t=PACK))
+        for n in range(1, PASSES * PACK - 1):
+            load_x(n // PACK, n % PACK)
+        load_w(0)
+        load_x(PASSES - 1, PACK - 1)
+        load_w(1)
 
         w2_scale = keep.tile([P, N], U8, name="w2_scale", align_bytes=64)
         w2_code = keep.tile([P, N], U32, name="w2_code", align_bytes=64)
@@ -68,32 +75,43 @@ def tile_picked_inorm_relu_e_kernel(tc, xT, w1, w2_words, w2_scales, gamma, offs
         nc.scalar.activation(neg_gamma[:], gamma_sb[:], ACT.Copy, scale=-1.0)
         nc.scalar.activation(factors[:, :, 0], gamma_sb[:], ACT.Copy)
 
-        x_code, x_scale = [], []
+        x_code = [keep.tile([P, S], U32, name=f"x_code{g}", align_bytes=64) for g in range(PASSES)]
+        x_scale = [keep.tile([P, S], U8, name=f"x_scale{g}", align_bytes=64) for g in range(PASSES)]
+        picked = {}
         for g in range(PASSES):
-            picked = [keep.tile([P, PACK, HALF], F32, name=f"picked{g}{u}") for u in range(2)]
-            for j in range(PACK):
-                for u in range(2):
-                    nc.vector.tensor_copy(picked[u][:, j, :], windows[g, j].indirect(offsets[:, 16 * u : 16 * (u + 1)]))
-            x_woven = keep.tile([P, S, PACK], BF16, name=f"x_woven{g}", align_bytes=64)
-            nc.scalar.copy(x_woven[:, :HALF], picked[0][:].rearrange("p j s -> p s j"))
-            nc.vector.tensor_copy(x_woven[:, HALF:], picked[1][:].rearrange("p j s -> p s j"))
-            code = keep.tile([P, S], U32, name=f"x_code{g}", align_bytes=64)
-            scale = keep.tile([P, S], U8, name=f"x_scale{g}", align_bytes=64)
-            nc.vector.quantize_mx(code[:].bitcast(FP8X4), scale[:], x_woven[:].rearrange("p s j -> p (s j)"))
-            x_code.append(code)
-            x_scale.append(scale)
+            for lo, hi, on_vector in X_PIECES:
+                picked[g, lo] = keep.tile([P, PACK, hi - lo], BF16, name=f"picked{g}_{lo}")
 
-        pieces = [(t, 0, S) for t in range(PACK - 1)] + [(PACK - 1, 0, HALF), (PACK - 1, HALF, S)]
+        def gather(g, j):
+            for lo, hi, on_vector in X_PIECES:
+                nc.vector.tensor_copy(picked[g, lo][:, j, :], planes[g, j][:].indirect(offsets[:, lo // 16 : hi // 16]))
+
+        def quantise_x(g):
+            woven = {}
+            for lo, hi, on_vector in X_PIECES:
+                woven[lo] = keep.tile([P, hi - lo, PACK], BF16, name=f"x_woven{g}_{lo}", align_bytes=64)
+                copy = nc.vector.tensor_copy if on_vector else nc.scalar.copy
+                copy(woven[lo][:], picked[g, lo][:].rearrange("p j s -> p s j"))
+            for lo, hi, on_vector in X_PIECES:
+                nc.vector.quantize_mx(
+                    x_code[g][:, lo:hi].bitcast(FP8X4), x_scale[g][:, lo:hi], woven[lo][:].rearrange("p s j -> p (s j)")
+                )
+
+        pieces = [(0, 0, S), (1, 0, S), (2, 0, HALF), (2, HALF, S), (3, 0, HALF), (3, HALF, S)]
         banks = {}
         for t, lo, hi in pieces:
-            banks[t, lo] = psum.tile([P, hi - lo], F32, name=f"h{t}_{lo}")
-        for g in range(PASSES):
+            banks[t, lo] = psum.tile([P, hi - lo], F32, name=f"h{t}_{lo}", tag=f"bank{t}_{lo}")
+
+        w_codes = {}
+
+        def first_layer(g):
             src = w_raw[g][:].rearrange("p j (m t) -> p m t j", t=PACK)
             for t0 in (0, 2):
                 dealt = keep.tile([P, 2, P, PACK], BF16, name=f"dealt{g}{t0}", align_bytes=64)
                 dst = dealt[:].rearrange("p t m j -> p m t j")
-                split = M_VECTOR_LATE if (g, t0) == (PASSES - 1, 2) else M_VECTOR
-                nc.vector.tensor_copy(dst[:, :split], src[:, :split, t0 : t0 + 2])
+                split = W_SPLITS[g, t0]
+                if split:
+                    nc.vector.tensor_copy(dst[:, :split], src[:, :split, t0 : t0 + 2])
                 nc.scalar.copy(dst[:, split:], src[:, split:, t0 : t0 + 2])
                 for t in (t0, t0 + 1):
                     code = keep.tile([P, P], U32, name=f"w_code{g}{t}", align_bytes=64)
@@ -101,6 +119,7 @@ def tile_picked_inorm_relu_e_kernel(tc, xT, w1, w2_words, w2_scales, gamma, offs
                     nc.vector.quantize_mx(
                         code[:].bitcast(FP8X4), scale[:], dealt[:, t - t0].rearrange("p m j -> p (m j)")
                     )
+                    w_codes[g, t] = (code, scale)
                     for tt, lo, hi in pieces:
                         if tt == t:
                             nc.tensor.matmul_mx(
@@ -113,12 +132,30 @@ def tile_picked_inorm_relu_e_kernel(tc, xT, w1, w2_words, w2_scales, gamma, offs
                                 stop=(g == PASSES - 1),
                             )
 
+        for j in range(PACK):
+            gather(0, j)
+        quantise_x(0)
+        for j in range(PACK - 1):
+            gather(1, j)
+        first_layer(0)
+        gather(1, PACK - 1)
+        quantise_x(1)
+        spare = psum.tile([P, PACK, QUARTER], F32, name="spare", tag="acc3")
+        for lo in (0, QUARTER):
+            for t in range(PACK):
+                nc.tensor.matmul_mx(
+                    spare[:, t, :], lhsT=w_codes[0, t][0][:].bitcast(FP8X4), lhsT_scale=w_codes[0, t][1][:],
+                    rhs=x_code[1][:, lo : lo + QUARTER].bitcast(FP8X4), rhs_scale=x_scale[1][:, lo : lo + QUARTER],
+                    start=True, stop=True,
+                )
+        first_layer(1)
+
         def h_cols(t, lo, hi):
             if (t, HALF) in banks and lo >= HALF:
                 return banks[t, HALF][:, lo - HALF : hi - HALF]
             return banks[t, 0][:, lo:hi]
 
-        stats = [keep.tile([P, 2, 6], F32, name=f"stats{t}") for t in range(PACK)]
+        stats = {t: keep.tile([P, 2, 6], F32, name=f"stats{t}") for t in range(1, PACK)}
         moments = [keep.tile([P, 2], F32, name=f"moments{t}") for t in range(PACK)]
         rstd = [keep.tile([P, 1], F32, name=f"rstd{t}") for t in range(PACK)]
         affine = [keep.tile([P, 2], F32, name=f"affine{t}") for t in range(PACK)]
@@ -127,11 +164,18 @@ def tile_picked_inorm_relu_e_kernel(tc, xT, w1, w2_words, w2_scales, gamma, offs
         def half_stats(t, u):
             nc.vector.bn_stats(stats[t][:, u, :], h_cols(t, u * HALF, (u + 1) * HALF))
 
+        h0 = keep.tile([P, S], F32, name="h0")
+        squares = keep.tile([P, S], BF16, name="squares")
+        sums = keep.tile([P, 2], F32, name="sums")
+
         def finish_stats(t):
             nc.vector.bn_aggr(moments[t][:], stats[t][:].rearrange("p u s -> p (u s)"))
             nc.scalar.activation(rstd[t][:], moments[t][:, 1:2], ACT.Abs_reciprocal_sqrt, bias=EPS)
             nc.scalar.activation(factors[:, t, 1:2], moments[t][:, 0:1], ACT.Copy, scale=neg_gamma[:, t : t + 1])
-            nc.scalar.activation(affine[t][:], factors[:, t, :], ACT.Copy, scale=rstd[t][:])
+
+        def scale_factors(t):
+            width = 1 if t == 0 else 2
+            nc.scalar.activation(affine[t][:, :width], factors[:, t, :width], ACT.Copy, scale=rstd[t][:])
 
         def normalise_scalar(t, u):
             nc.scalar.activation(
@@ -139,40 +183,69 @@ def tile_picked_inorm_relu_e_kernel(tc, xT, w1, w2_words, w2_scales, gamma, offs
                 scale=affine[t][:, 0:1], bias=affine[t][:, 1:2],
             )
 
-        half_stats(0, 0)
-        half_stats(0, 1)
-        for t in range(1, PACK):
-            half_stats(t, 0)
-            finish_stats(t - 1)
-            half_stats(t, 1)
-            normalise_scalar(t - 1, 0)
-            normalise_scalar(t - 1, 1)
-        last = PACK - 1
-        finish_stats(last)
-        nc.vector.tensor_scalar(
-            z_planes[0][:, last, :], h_cols(last, 0, HALF), affine[last][:, 0:1], affine[last][:, 1:2], ALU.mult, ALU.add
-        )
-        normalise_scalar(last, 1)
+        def normalise_vector(t, lo, hi):
+            u = lo // HALF
+            src = h0[:, lo:hi] if t == 0 else h_cols(t, lo, hi)
+            nc.vector.tensor_scalar(
+                z_planes[u][:, t, lo - u * HALF : hi - u * HALF], src,
+                moments[t][:, 0:1], affine[t][:, 0:1], ALU.add if t == 0 else ALU.subtract, ALU.mult,
+            )
 
-        for u in range(2):
-            woven = keep.tile([P, HALF, PACK], BF16, name=f"woven{u}", align_bytes=64)
-            src = z_planes[u][:].rearrange("p t s -> p s t")
-            if u == 0:
-                nc.vector.tensor_scalar_max(woven[:], src, 0.0)
-            else:
-                nc.vector.tensor_copy(woven[:, :P], src[:, :P])
-                nc.scalar.copy(woven[:, P:], src[:, P:])
-            code = keep.tile([P, HALF], U32, name=f"z_code{u}", align_bytes=64)
-            scale = keep.tile([P, HALF], U8, name=f"z_scale{u}", align_bytes=64)
-            nc.vector.quantize_mx(code[:].bitcast(FP8X4), scale[:], woven[:].rearrange("p s t -> p (s t)"))
-            acc = psum.tile([P, HALF], F32, name=f"acc{u}")
+        nc.scalar.activation(h0[:], banks[0, 0][:], ACT.Copy, accum_out=sums[:, 0:1])
+        nc.scalar.activation(moments[0][:, 0:1], sums[:, 0:1], ACT.Copy, scale=-1.0 / S)
+        nc.scalar.activation(squares[:], h0[:], ACT.Square, bias=moments[0][:, 0:1], accum_out=sums[:, 1:2])
+        nc.scalar.activation(rstd[0][:], sums[:, 1:2], ACT.Abs_reciprocal_sqrt, scale=1.0 / S, bias=EPS)
+        half_stats(1, 0)
+        half_stats(1, 1)
+        half_stats(2, 0)
+        finish_stats(1)
+        scale_factors(0)
+        scale_factors(1)
+        half_stats(2, 1)
+        half_stats(3, 0)
+        normalise_scalar(1, 0)
+        finish_stats(2)
+        normalise_scalar(1, 1)
+        scale_factors(2)
+        half_stats(3, 1)
+        finish_stats(3)
+        normalise_vector(0, 0, HALF)
+        normalise_vector(0, HALF, S)
+        scale_factors(3)
+        normalise_vector(2, 0, HALF)
+        normalise_scalar(2, 1)
+        normalise_vector(3, 0, QUARTER)
+        normalise_vector(3, QUARTER, HALF)
+        normalise_scalar(3, 1)
+
+        woven = [keep.tile([P, QUARTER, PACK], BF16, name=f"woven{c}", align_bytes=64) for c in range(4)]
+
+        def weave(c):
+            src = z_planes[c // 2][:, :, (c % 2) * QUARTER : (c % 2 + 1) * QUARTER].rearrange("p t s -> p s t")
+            split = Z_SPLITS[c]
+            if split > 0:
+                nc.vector.tensor_scalar_max(woven[c][:, :split], src[:, :split], 0.0)
+            if split < QUARTER:
+                nc.scalar.activation(woven[c][:, split:], src[:, split:], ACT.Relu)
+
+        def second_layer(c):
+            code = keep.tile([P, QUARTER], U32, name=f"z_code{c}", align_bytes=64)
+            scale = keep.tile([P, QUARTER], U8, name=f"z_scale{c}", align_bytes=64)
+            nc.vector.quantize_mx(code[:].bitcast(FP8X4), scale[:], woven[c][:].rearrange("p s t -> p (s t)"))
+            acc = psum.tile([P, QUARTER], F32, name=f"acc{c}", tag=f"acc{c}" if c >= 2 else f"bank{c}_0")
             nc.tensor.matmul_mx(
                 acc[:], lhsT=w2_code[:].bitcast(FP8X4), lhsT_scale=w2_scale[:],
                 rhs=code[:].bitcast(FP8X4), rhs_scale=scale[:], start=True, stop=True,
             )
-            result = keep.tile([P, HALF], F32, name=f"result{u}")
-            if u == 0:
-                nc.scalar.copy(result[:], acc[:])
-            else:
-                nc.vector.tensor_copy(result[:], acc[:])
-            nc.sync.dma_start(out[:, u * HALF : (u + 1) * HALF], result[:])
+            result = keep.tile([P, QUARTER], F32, name=f"result{c}")
+            nc.scalar.copy(result[:], acc[:])
+            nc.sync.dma_start(out[:, c * QUARTER : (c + 1) * QUARTER], result[:])
+
+        weave(0)
+        weave(3)
+        weave(1)
+        second_layer(0)
+        weave(2)
+        second_layer(1)
+        second_layer(3)
+        second_layer(2)

@@ -22,7 +22,7 @@ K_PASS = P * PACK
 PASSES = K // K_PASS
 HALF = S // 2
 QUARTER = S // 4
-W_SPLITS = {(0, 0): 0, (0, 2): 96, (1, 0): 56, (1, 2): 72}
+W_SPLITS = (72, 84)
 Z_SPLITS = (128, 128, 64, 0)
 X_PIECES = ((0, 128, False), (128, 256, False), (256, 384, True), (384, 512, True))
 
@@ -53,8 +53,8 @@ def tile_picked_inorm_relu_e_kernel(tc, xT, w1, w2_words, w2_scales, gamma, offs
         nc.sync.dma_start(gamma_sb[:], gamma.rearrange("(p t) o -> p (t o)", t=PACK))
         for n in range(1, PASSES * PACK - 1):
             load_x(n // PACK, n % PACK)
-        load_w(0)
         load_x(PASSES - 1, PACK - 1)
+        load_w(0)
         load_w(1)
 
         w2_scale = keep.tile([P, N], U8, name="w2_scale", align_bytes=64)
@@ -102,53 +102,35 @@ def tile_picked_inorm_relu_e_kernel(tc, xT, w1, w2_words, w2_scales, gamma, offs
         for t, lo, hi in pieces:
             banks[t, lo] = psum.tile([P, hi - lo], F32, name=f"h{t}_{lo}", tag=f"bank{t}_{lo}")
 
-        w_codes = {}
-
         def first_layer(g):
-            src = w_raw[g][:].rearrange("p j (m t) -> p m t j", t=PACK)
-            for t0 in (0, 2):
-                dealt = keep.tile([P, 2, P, PACK], BF16, name=f"dealt{g}{t0}", align_bytes=64)
-                dst = dealt[:].rearrange("p t m j -> p m t j")
-                split = W_SPLITS[g, t0]
-                if split:
-                    nc.vector.tensor_copy(dst[:, :split], src[:, :split, t0 : t0 + 2])
-                nc.scalar.copy(dst[:, split:], src[:, split:, t0 : t0 + 2])
-                for t in (t0, t0 + 1):
-                    code = keep.tile([P, P], U32, name=f"w_code{g}{t}", align_bytes=64)
-                    scale = keep.tile([P, P], U8, name=f"w_scale{g}{t}", align_bytes=64)
-                    nc.vector.quantize_mx(
-                        code[:].bitcast(FP8X4), scale[:], dealt[:, t - t0].rearrange("p m j -> p (m j)")
-                    )
-                    w_codes[g, t] = (code, scale)
-                    for tt, lo, hi in pieces:
-                        if tt == t:
-                            nc.tensor.matmul_mx(
-                                banks[t, lo][:],
-                                lhsT=code[:].bitcast(FP8X4),
-                                lhsT_scale=scale[:],
-                                rhs=x_code[g][:, lo:hi].bitcast(FP8X4),
-                                rhs_scale=x_scale[g][:, lo:hi],
-                                start=(g == 0),
-                                stop=(g == PASSES - 1),
-                            )
-
-        for j in range(PACK):
-            gather(0, j)
-        quantise_x(0)
-        for j in range(PACK - 1):
-            gather(1, j)
-        first_layer(0)
-        gather(1, PACK - 1)
-        quantise_x(1)
-        spare = psum.tile([P, PACK, QUARTER], F32, name="spare", tag="acc3")
-        for lo in (0, QUARTER):
+            src = w_raw[g][:].rearrange("p j (m t) -> p m j t", t=PACK)
+            dealt = keep.tile([P, PACK, P, PACK], BF16, name=f"dealt{g}", align_bytes=64)
+            dst = dealt[:].rearrange("p t m j -> p m j t")
+            split = W_SPLITS[g]
+            nc.vector.tensor_copy(dst[:, :split], src[:, :split])
+            nc.scalar.copy(dst[:, split:], src[:, split:])
             for t in range(PACK):
-                nc.tensor.matmul_mx(
-                    spare[:, t, :], lhsT=w_codes[0, t][0][:].bitcast(FP8X4), lhsT_scale=w_codes[0, t][1][:],
-                    rhs=x_code[1][:, lo : lo + QUARTER].bitcast(FP8X4), rhs_scale=x_scale[1][:, lo : lo + QUARTER],
-                    start=True, stop=True,
-                )
-        first_layer(1)
+                code = keep.tile([P, P], U32, name=f"w_code{g}{t}", align_bytes=64)
+                scale = keep.tile([P, P], U8, name=f"w_scale{g}{t}", align_bytes=64)
+                nc.vector.quantize_mx(code[:].bitcast(FP8X4), scale[:], dealt[:, t].rearrange("p m j -> p (m j)"))
+                for tt, lo, hi in pieces:
+                    if tt == t:
+                        nc.tensor.matmul_mx(
+                            banks[t, lo][:],
+                            lhsT=code[:].bitcast(FP8X4),
+                            lhsT_scale=scale[:],
+                            rhs=x_code[g][:, lo:hi].bitcast(FP8X4),
+                            rhs_scale=x_scale[g][:, lo:hi],
+                            start=(g == 0),
+                            stop=(g == PASSES - 1),
+                        )
+
+        for g in range(PASSES):
+            for j in range(PACK):
+                gather(g, j)
+            quantise_x(g)
+        for g in range(PASSES):
+            first_layer(g)
 
         def h_cols(t, lo, hi):
             if (t, HALF) in banks and lo >= HALF:

@@ -23,6 +23,7 @@ PASSES = K // K_PASS
 HALF = S // 2
 QUARTER = S // 4
 W_SPLITS = (72, 84)
+X_LOADS = ((0, 0, 2), (0, 2, 2), (1, 0, 2), (1, 2, 1), (1, 3, 1))
 Z_SPLITS = (128, 128, 64, 0)
 X_PIECES = ((0, 128, False), (128, 256, False), (256, 384, True), (384, 512, True))
 
@@ -35,25 +36,26 @@ def tile_picked_inorm_relu_e_kernel(tc, xT, w1, w2_words, w2_scales, gamma, offs
 
         offsets = keep.tile([P, S // 16], U16, name="offsets")
         gamma_sb = keep.tile([P, PACK], F32, name="gamma_sb")
-        x_rows = xT.rearrange("(g p j) c -> g j p c", p=P, j=PACK)
+        x_rows = xT.rearrange("(g p j) c -> g p j c", p=P, j=PACK)
         w_rows = w1.rearrange("(g p j) c -> g p j c", p=P, j=PACK)
         planes = {}
         w_raw = {}
 
-        def load_x(g, j):
-            planes[g, j] = keep.tile([P, T], F32, name=f"plane{g}{j}")
-            nc.sync.dma_start(planes[g, j][:], x_rows[g, j])
+        def load_x(g, j, count):
+            rows = keep.tile([P, count, T], F32, name=f"rows{g}{j}")
+            nc.sync.dma_start(rows[:], x_rows[g, :, j : j + count])
+            for i in range(count):
+                planes[g, j + i] = rows[:, i, :]
 
         def load_w(g):
             w_raw[g] = keep.tile([P, PACK, H], F32, name=f"w_raw{g}")
             nc.sync.dma_start(w_raw[g][:], w_rows[g])
 
-        load_x(0, 0)
+        load_x(*X_LOADS[0])
         nc.sync.dma_start(offsets[:], offs)
         nc.sync.dma_start(gamma_sb[:], gamma.rearrange("(p t) o -> p (t o)", t=PACK))
-        for n in range(1, PASSES * PACK - 1):
-            load_x(n // PACK, n % PACK)
-        load_x(PASSES - 1, PACK - 1)
+        for g, j, count in X_LOADS[1:]:
+            load_x(g, j, count)
         load_w(0)
         load_w(1)
 
@@ -77,21 +79,21 @@ def tile_picked_inorm_relu_e_kernel(tc, xT, w1, w2_words, w2_scales, gamma, offs
 
         x_code = [keep.tile([P, S], U32, name=f"x_code{g}", align_bytes=64) for g in range(PASSES)]
         x_scale = [keep.tile([P, S], U8, name=f"x_scale{g}", align_bytes=64) for g in range(PASSES)]
-        picked = {}
-        for g in range(PASSES):
-            for lo, hi, on_vector in X_PIECES:
-                picked[g, lo] = keep.tile([P, PACK, hi - lo], BF16, name=f"picked{g}_{lo}")
+        picked = [keep.tile([P, 4, PACK, QUARTER], BF16, name=f"picked{g}") for g in range(PASSES)]
 
         def gather(g, j):
-            for lo, hi, on_vector in X_PIECES:
-                nc.vector.tensor_copy(picked[g, lo][:, j, :], planes[g, j][:].indirect(offsets[:, lo // 16 : hi // 16]))
+            if (g, j) == (PASSES - 1, PACK - 1):
+                for q in range(4):
+                    nc.vector.tensor_copy(picked[g][:, q, j, :], planes[g, j].indirect(offsets[:, q * 8 : (q + 1) * 8]))
+            else:
+                nc.vector.tensor_copy(picked[g][:, :, j, :], planes[g, j].indirect(offsets[:]))
 
         def quantise_x(g):
             woven = {}
             for lo, hi, on_vector in X_PIECES:
                 woven[lo] = keep.tile([P, hi - lo, PACK], BF16, name=f"x_woven{g}_{lo}", align_bytes=64)
                 copy = nc.vector.tensor_copy if on_vector else nc.scalar.copy
-                copy(woven[lo][:], picked[g, lo][:].rearrange("p j s -> p s j"))
+                copy(woven[lo][:], picked[g][:, lo // QUARTER].rearrange("p j s -> p s j"))
             for lo, hi, on_vector in X_PIECES:
                 nc.vector.quantize_mx(
                     x_code[g][:, lo:hi].bitcast(FP8X4), x_scale[g][:, lo:hi], woven[lo][:].rearrange("p s j -> p (s j)")

@@ -22,7 +22,8 @@ K_PASS = P * PACK
 PASSES = K // K_PASS
 HALF = S // 2
 QUARTER = S // 4
-W_SPLITS = (72, 84)
+W_PIECES = ((0, 0, 128), (1, 0, 48), (1, 48, 128))
+W_DEALS = ((0, 0, 0, 2, 64), (0, 0, 2, 4, 64), (1, 0, 0, 4, 0), (1, 48, 0, 4, 54))
 X_LOADS = ((0, 0, 2), (0, 2, 2), (1, 0, 2), (1, 2, 1), (1, 3, 1))
 Z_SPLITS = (128, 128, 64, 0)
 X_PIECES = ((0, 128, False), (128, 256, False), (256, 384, True), (384, 512, True))
@@ -47,17 +48,17 @@ def tile_picked_inorm_relu_e_kernel(tc, xT, w1, w2_words, w2_scales, gamma, offs
             for i in range(count):
                 planes[g, j + i] = rows[:, i, :]
 
-        def load_w(g):
-            w_raw[g] = keep.tile([P, PACK, H], F32, name=f"w_raw{g}")
-            nc.sync.dma_start(w_raw[g][:], w_rows[g])
+        def load_w(g, lo, hi):
+            w_raw[g, lo] = keep.tile([P, PACK, PACK * (hi - lo)], F32, name=f"w_raw{g}_{lo}")
+            nc.sync.dma_start(w_raw[g, lo][:], w_rows[g, :, :, PACK * lo : PACK * hi])
 
         load_x(*X_LOADS[0])
         nc.sync.dma_start(offsets[:], offs)
         nc.sync.dma_start(gamma_sb[:], gamma.rearrange("(p t) o -> p (t o)", t=PACK))
         for g, j, count in X_LOADS[1:]:
             load_x(g, j, count)
-        load_w(0)
-        load_w(1)
+        for g, lo, hi in W_PIECES:
+            load_w(g, lo, hi)
 
         w2_scale = keep.tile([P, N], U8, name="w2_scale", align_bytes=64)
         w2_code = keep.tile([P, N], U32, name="w2_code", align_bytes=64)
@@ -104,35 +105,45 @@ def tile_picked_inorm_relu_e_kernel(tc, xT, w1, w2_words, w2_scales, gamma, offs
         for t, lo, hi in pieces:
             banks[t, lo] = psum.tile([P, hi - lo], F32, name=f"h{t}_{lo}", tag=f"bank{t}_{lo}")
 
-        def first_layer(g):
-            src = w_raw[g][:].rearrange("p j (m t) -> p m j t", t=PACK)
-            dealt = keep.tile([P, PACK, P, PACK], BF16, name=f"dealt{g}", align_bytes=64)
-            dst = dealt[:].rearrange("p t m j -> p m j t")
-            split = W_SPLITS[g]
-            nc.vector.tensor_copy(dst[:, :split], src[:, :split])
-            nc.scalar.copy(dst[:, split:], src[:, split:])
-            for t in range(PACK):
-                code = keep.tile([P, P], U32, name=f"w_code{g}{t}", align_bytes=64)
-                scale = keep.tile([P, P], U8, name=f"w_scale{g}{t}", align_bytes=64)
-                nc.vector.quantize_mx(code[:].bitcast(FP8X4), scale[:], dealt[:, t].rearrange("p m j -> p (m j)"))
-                for tt, lo, hi in pieces:
-                    if tt == t:
-                        nc.tensor.matmul_mx(
-                            banks[t, lo][:],
-                            lhsT=code[:].bitcast(FP8X4),
-                            lhsT_scale=scale[:],
-                            rhs=x_code[g][:, lo:hi].bitcast(FP8X4),
-                            rhs_scale=x_scale[g][:, lo:hi],
-                            start=(g == 0),
-                            stop=(g == PASSES - 1),
-                        )
+        dealt = [keep.tile([P, PACK, P, PACK], BF16, name=f"dealt{g}", align_bytes=64) for g in range(PASSES)]
+
+        def deal(g, lo, t_lo, t_hi, on_vector):
+            src = w_raw[g, lo][:].rearrange("p j (m t) -> p m j t", t=PACK)[:, :, :, t_lo:t_hi]
+            dst = dealt[g][:].rearrange("p t m j -> p m j t")[:, lo : lo + src.shape[1], :, t_lo:t_hi]
+            if on_vector:
+                nc.vector.tensor_copy(dst[:, :on_vector], src[:, :on_vector])
+            nc.scalar.copy(dst[:, on_vector:], src[:, on_vector:])
+
+        def first_layer(g, t):
+            code = keep.tile([P, P], U32, name=f"w_code{g}{t}", align_bytes=64)
+            scale = keep.tile([P, P], U8, name=f"w_scale{g}{t}", align_bytes=64)
+            nc.vector.quantize_mx(code[:].bitcast(FP8X4), scale[:], dealt[g][:, t].rearrange("p m j -> p (m j)"))
+            for tt, lo, hi in pieces:
+                if tt == t:
+                    nc.tensor.matmul_mx(
+                        banks[t, lo][:],
+                        lhsT=code[:].bitcast(FP8X4),
+                        lhsT_scale=scale[:],
+                        rhs=x_code[g][:, lo:hi].bitcast(FP8X4),
+                        rhs_scale=x_scale[g][:, lo:hi],
+                        start=(g == 0),
+                        stop=(g == PASSES - 1),
+                    )
 
         for g in range(PASSES):
             for j in range(PACK):
                 gather(g, j)
             quantise_x(g)
-        for g in range(PASSES):
-            first_layer(g)
+        deal(*W_DEALS[0])
+        first_layer(0, 0)
+        first_layer(0, 1)
+        deal(*W_DEALS[1])
+        first_layer(0, 2)
+        first_layer(0, 3)
+        deal(*W_DEALS[2])
+        deal(*W_DEALS[3])
+        for t in range(PACK):
+            first_layer(1, t)
 
         def h_cols(t, lo, hi):
             if (t, HALF) in banks and lo >= HALF:

@@ -22,8 +22,8 @@ K_PASS = P * PACK
 PASSES = K // K_PASS
 HALF = S // 2
 QUARTER = S // 4
-W_PIECES = ((0, 0, 128), (1, 0, 48), (1, 48, 128))
-W_DEALS = ((0, 0, 0, 2, 64), (0, 0, 2, 4, 64), (1, 0, 0, 4, 0), (1, 48, 0, 4, 54))
+W_PIECES = ((0, 0, 128), (1, 0, 128))
+W_DEALS = ((0, 0, 0, 2, 64), (0, 0, 2, 4, 64), (1, 0, 0, 4, 84))
 X_LOADS = ((0, 0, 2), (0, 2, 2), (1, 0, 2), (1, 2, 1), (1, 3, 1))
 Z_SPLITS = (128, 128, 64, 0)
 X_PIECES = ((0, 128, False), (128, 256, False), (256, 384, True), (384, 512, True))
@@ -134,6 +134,11 @@ def tile_picked_inorm_relu_e_kernel(tc, xT, w1, w2_words, w2_scales, gamma, offs
             for j in range(PACK):
                 gather(g, j)
             quantise_x(g)
+        spare = psum.tile([P, S], F32, name="spare", tag="acc3")
+        nc.tensor.matmul_mx(
+            spare[:], lhsT=x_code[1][:, S - P :].bitcast(FP8X4), lhsT_scale=x_scale[1][:, S - P :],
+            rhs=x_code[0][:].bitcast(FP8X4), rhs_scale=x_scale[0][:], start=True, stop=True,
+        )
         deal(*W_DEALS[0])
         first_layer(0, 0)
         first_layer(0, 1)
@@ -141,7 +146,6 @@ def tile_picked_inorm_relu_e_kernel(tc, xT, w1, w2_words, w2_scales, gamma, offs
         first_layer(0, 2)
         first_layer(0, 3)
         deal(*W_DEALS[2])
-        deal(*W_DEALS[3])
         for t in range(PACK):
             first_layer(1, t)
 

@@ -23,7 +23,7 @@ PASSES = K // K_PASS
 HALF = S // 2
 QUARTER = S // 4
 W_PIECES = ((0, 0, 128), (1, 0, 128))
-W_DEALS = ((0, 0, 0, 2, 64), (0, 0, 2, 4, 64), (1, 0, 0, 4, 84))
+W_DEALS = ((0, 0, 0, 4, 72), (1, 0, 0, 2, 80), (1, 0, 2, 4, 52))
 X_LOADS = ((0, 0, 2), (0, 2, 2), (1, 0, 2), (1, 2, 1), (1, 3, 1))
 Z_SPLITS = (128, 128, 64, 0)
 X_PIECES = ((0, 128, False), (128, 256, False), (256, 384, True), (384, 512, True))
@@ -100,10 +100,8 @@ def tile_picked_inorm_relu_e_kernel(tc, xT, w1, w2_words, w2_scales, gamma, offs
                     x_code[g][:, lo:hi].bitcast(FP8X4), x_scale[g][:, lo:hi], woven[lo][:].rearrange("p s j -> p (s j)")
                 )
 
-        pieces = [(0, 0, S), (1, 0, S), (2, 0, HALF), (2, HALF, S), (3, 0, HALF), (3, HALF, S)]
+        pieces = [(t, lo, lo + HALF) for t in range(PACK) for lo in (0, HALF)]
         banks = {}
-        for t, lo, hi in pieces:
-            banks[t, lo] = psum.tile([P, hi - lo], F32, name=f"h{t}_{lo}", tag=f"bank{t}_{lo}")
 
         dealt = [keep.tile([P, PACK, P, PACK], BF16, name=f"dealt{g}", align_bytes=64) for g in range(PASSES)]
 
@@ -134,20 +132,18 @@ def tile_picked_inorm_relu_e_kernel(tc, xT, w1, w2_words, w2_scales, gamma, offs
             for j in range(PACK):
                 gather(g, j)
             quantise_x(g)
-        spare = psum.tile([P, S], F32, name="spare", tag="acc3")
-        nc.tensor.matmul_mx(
-            spare[:], lhsT=x_code[1][:, S - P :].bitcast(FP8X4), lhsT_scale=x_scale[1][:, S - P :],
-            rhs=x_code[0][:].bitcast(FP8X4), rhs_scale=x_scale[0][:], start=True, stop=True,
-        )
-        deal(*W_DEALS[0])
-        first_layer(0, 0)
-        first_layer(0, 1)
-        deal(*W_DEALS[1])
-        first_layer(0, 2)
-        first_layer(0, 3)
-        deal(*W_DEALS[2])
-        for t in range(PACK):
-            first_layer(1, t)
+        spare = psum.tile([P, S], F32, name="spare", tag=f"bank{PACK - 1}_{HALF}")
+        for lo in (0, QUARTER):
+            nc.tensor.matmul_mx(
+                spare[:], lhsT=x_code[1][:, lo : lo + P].bitcast(FP8X4), lhsT_scale=x_scale[1][:, lo : lo + P],
+                rhs=x_code[0][:].bitcast(FP8X4), rhs_scale=x_scale[0][:], start=True, stop=True,
+            )
+        for t, lo, hi in pieces:
+            banks[t, lo] = psum.tile([P, hi - lo], F32, name=f"h{t}_{lo}", tag=f"bank{t}_{lo}")
+        for g, lo, t_lo, t_hi, on_vector in W_DEALS:
+            deal(g, lo, t_lo, t_hi, on_vector)
+            for t in range(t_lo, t_hi):
+                first_layer(g, t)
 
         def h_cols(t, lo, hi):
             if (t, HALF) in banks and lo >= HALF:
@@ -165,7 +161,8 @@ def tile_picked_inorm_relu_e_kernel(tc, xT, w1, w2_words, w2_scales, gamma, offs
 
         h0 = keep.tile([P, S], F32, name="h0")
         squares = keep.tile([P, S], BF16, name="squares")
-        sums = keep.tile([P, 2], F32, name="sums")
+        sums = keep.tile([P, 3], F32, name="sums")
+        scaled_sums = keep.tile([P, 2], F32, name="scaled_sums")
 
         def finish_stats(t):
             nc.vector.bn_aggr(moments[t][:], stats[t][:].rearrange("p u s -> p (u s)"))
@@ -190,10 +187,11 @@ def tile_picked_inorm_relu_e_kernel(tc, xT, w1, w2_words, w2_scales, gamma, offs
                 moments[t][:, 0:1], affine[t][:, 0:1], ALU.add if t == 0 else ALU.subtract, ALU.mult,
             )
 
-        nc.scalar.activation(h0[:], banks[0, 0][:], ACT.Copy, accum_out=sums[:, 0:1])
-        nc.scalar.activation(moments[0][:, 0:1], sums[:, 0:1], ACT.Copy, scale=-1.0 / S)
-        nc.scalar.activation(squares[:], h0[:], ACT.Square, bias=moments[0][:, 0:1], accum_out=sums[:, 1:2])
-        nc.scalar.activation(rstd[0][:], sums[:, 1:2], ACT.Abs_reciprocal_sqrt, scale=1.0 / S, bias=EPS)
+        for u in range(2):
+            nc.scalar.activation(h0[:, u * HALF : (u + 1) * HALF], banks[0, u * HALF][:], ACT.Copy, accum_out=sums[:, u : u + 1])
+        nc.scalar.activation(scaled_sums[:], sums[:, 0:2], ACT.Copy, scale=-1.0 / S, accum_out=moments[0][:, 0:1])
+        nc.scalar.activation(squares[:], h0[:], ACT.Square, bias=moments[0][:, 0:1], accum_out=sums[:, 2:3])
+        nc.scalar.activation(rstd[0][:], sums[:, 2:3], ACT.Abs_reciprocal_sqrt, scale=1.0 / S, bias=EPS)
         half_stats(1, 0)
         half_stats(1, 1)
         half_stats(2, 0)
@@ -231,7 +229,7 @@ def tile_picked_inorm_relu_e_kernel(tc, xT, w1, w2_words, w2_scales, gamma, offs
             code = keep.tile([P, QUARTER], U32, name=f"z_code{c}", align_bytes=64)
             scale = keep.tile([P, QUARTER], U8, name=f"z_scale{c}", align_bytes=64)
             nc.vector.quantize_mx(code[:].bitcast(FP8X4), scale[:], woven[c][:].rearrange("p s t -> p (s t)"))
-            acc = psum.tile([P, QUARTER], F32, name=f"acc{c}", tag=f"acc{c}" if c >= 2 else f"bank{c}_0")
+            acc = psum.tile([P, QUARTER], F32, name=f"acc{c}", tag=f"bank{c // 2}_{(c % 2) * HALF}")
             nc.tensor.matmul_mx(
                 acc[:], lhsT=w2_code[:].bitcast(FP8X4), lhsT_scale=w2_scale[:],
                 rhs=code[:].bitcast(FP8X4), rhs_scale=scale[:], start=True, stop=True,

@@ -25,6 +25,7 @@ QUARTER = S // 4
 W_PIECES = ((0, 0, 128), (1, 0, 128))
 W_DEALS = ((0, 0, 0, 4, 72), (1, 0, 0, 2, 80), (1, 0, 2, 4, 52))
 X_LOADS = ((0, 0, 2), (0, 2, 2), (1, 0, 2), (1, 2, 1), (1, 3, 1))
+WALK = 4
 Z_SPLITS = (128, 128, 64, 0)
 X_PIECES = ((0, 128, False), (128, 256, False), (256, 384, True), (384, 512, True))
 
@@ -54,11 +55,11 @@ def tile_picked_inorm_relu_e_kernel(tc, xT, w1, w2_words, w2_scales, gamma, offs
 
         load_x(*X_LOADS[0])
         nc.sync.dma_start(offsets[:], offs)
-        nc.sync.dma_start(gamma_sb[:], gamma.rearrange("(p t) o -> p (t o)", t=PACK))
         for g, j, count in X_LOADS[1:]:
             load_x(g, j, count)
         for g, lo, hi in W_PIECES:
             load_w(g, lo, hi)
+        nc.sync.dma_start(gamma_sb[:], gamma.rearrange("(p t) o -> p (t o)", t=PACK))
 
         w2_scale = keep.tile([P, N], U8, name="w2_scale", align_bytes=64)
         w2_code = keep.tile([P, N], U32, name="w2_code", align_bytes=64)
@@ -75,8 +76,6 @@ def tile_picked_inorm_relu_e_kernel(tc, xT, w1, w2_words, w2_scales, gamma, offs
         nc.scalar.activation(warm_out[:], warm_in[:], ACT.Abs_reciprocal_sqrt)
         neg_gamma = keep.tile([P, PACK], F32, name="neg_gamma")
         factors = keep.tile([P, PACK, 2], F32, name="factors")
-        nc.scalar.activation(neg_gamma[:], gamma_sb[:], ACT.Copy, scale=-1.0)
-        nc.scalar.activation(factors[:, :, 0], gamma_sb[:], ACT.Copy)
 
         x_code = [keep.tile([P, S], U32, name=f"x_code{g}", align_bytes=64) for g in range(PASSES)]
         x_scale = [keep.tile([P, S], U8, name=f"x_scale{g}", align_bytes=64) for g in range(PASSES)]
@@ -94,7 +93,10 @@ def tile_picked_inorm_relu_e_kernel(tc, xT, w1, w2_words, w2_scales, gamma, offs
             for lo, hi, on_vector in X_PIECES:
                 woven[lo] = keep.tile([P, hi - lo, PACK], BF16, name=f"x_woven{g}_{lo}", align_bytes=64)
                 copy = nc.vector.tensor_copy if on_vector else nc.scalar.copy
-                copy(woven[lo][:], picked[g][:, lo // QUARTER].rearrange("p j s -> p s j"))
+                copy(
+                    woven[lo][:].rearrange("p (c i) j -> p c j i", i=WALK),
+                    picked[g][:, lo // QUARTER].rearrange("p j (c i) -> p c j i", i=WALK),
+                )
             for lo, hi, on_vector in X_PIECES:
                 nc.vector.quantize_mx(
                     x_code[g][:, lo:hi].bitcast(FP8X4), x_scale[g][:, lo:hi], woven[lo][:].rearrange("p s j -> p (s j)")
@@ -144,6 +146,9 @@ def tile_picked_inorm_relu_e_kernel(tc, xT, w1, w2_words, w2_scales, gamma, offs
             deal(g, lo, t_lo, t_hi, on_vector)
             for t in range(t_lo, t_hi):
                 first_layer(g, t)
+
+        nc.scalar.activation(neg_gamma[:], gamma_sb[:], ACT.Copy, scale=-1.0)
+        nc.scalar.activation(factors[:, :, 0], gamma_sb[:], ACT.Copy)
 
         def h_cols(t, lo, hi):
             if (t, HALF) in banks and lo >= HALF:
@@ -218,12 +223,13 @@ def tile_picked_inorm_relu_e_kernel(tc, xT, w1, w2_words, w2_scales, gamma, offs
         woven = [keep.tile([P, QUARTER, PACK], BF16, name=f"woven{c}", align_bytes=64) for c in range(4)]
 
         def weave(c):
-            src = z_planes[c // 2][:, :, (c % 2) * QUARTER : (c % 2 + 1) * QUARTER].rearrange("p t s -> p s t")
-            split = Z_SPLITS[c]
+            src = z_planes[c // 2][:, :, (c % 2) * QUARTER : (c % 2 + 1) * QUARTER].rearrange("p t (c i) -> p c t i", i=WALK)
+            dst = woven[c][:].rearrange("p (c i) t -> p c t i", i=WALK)
+            split = Z_SPLITS[c] // WALK
             if split > 0:
-                nc.vector.tensor_scalar_max(woven[c][:, :split], src[:, :split], 0.0)
-            if split < QUARTER:
-                nc.scalar.activation(woven[c][:, split:], src[:, split:], ACT.Relu)
+                nc.vector.tensor_scalar_max(dst[:, :split], src[:, :split], 0.0)
+            if split < QUARTER // WALK:
+                nc.scalar.activation(dst[:, split:], src[:, split:], ACT.Relu)
 
         def second_layer(c):
             code = keep.tile([P, QUARTER], U32, name=f"z_code{c}", align_bytes=64)
@@ -235,7 +241,7 @@ def tile_picked_inorm_relu_e_kernel(tc, xT, w1, w2_words, w2_scales, gamma, offs
                 rhs=code[:].bitcast(FP8X4), rhs_scale=scale[:], start=True, stop=True,
             )
             result = keep.tile([P, QUARTER], F32, name=f"result{c}")
-            nc.scalar.copy(result[:], acc[:])
+            (nc.vector.tensor_copy if c == 2 else nc.scalar.copy)(result[:], acc[:])
             nc.sync.dma_start(out[:, c * QUARTER : (c + 1) * QUARTER], result[:])
 
         weave(0)

@@ -5,6 +5,7 @@ import concourse.mybir as mybir
 K, T, S, H, N = 1024, 2048, 512, 512, 128
 FLOPS = 2 * K * H * S + 2 * H * N * S
 EPS = 1e-5
+TINY = 2.0**-100
 
 F32 = mybir.dt.float32
 BF16 = mybir.dt.bfloat16
@@ -26,7 +27,7 @@ W_PIECES = ((0, 0, 128), (1, 0, 128))
 W_DEALS = ((0, 0, 0, 4, 72), (1, 0, 0, 2, 80), (1, 0, 2, 4, 52))
 X_LOADS = ((0, 0, 2), (0, 2, 2), (1, 0, 2), (1, 2, 1), (1, 3, 1))
 WALK = 4
-Z_SPLITS = (128, 128, 64, 0)
+Z_SPLITS = (128, 128, 40, 0)
 X_PIECES = ((0, 128, False), (128, 256, False), (256, 384, True), (384, 512, True))
 
 
@@ -53,13 +54,13 @@ def tile_picked_inorm_relu_e_kernel(tc, xT, w1, w2_words, w2_scales, gamma, offs
             w_raw[g, lo] = keep.tile([P, PACK, PACK * (hi - lo)], F32, name=f"w_raw{g}_{lo}")
             nc.sync.dma_start(w_raw[g, lo][:], w_rows[g, :, :, PACK * lo : PACK * hi])
 
+        nc.scalar.dma_start(gamma_sb[:], gamma.rearrange("(p t) o -> p (t o)", t=PACK))
         load_x(*X_LOADS[0])
         nc.sync.dma_start(offsets[:], offs)
         for g, j, count in X_LOADS[1:]:
             load_x(g, j, count)
         for g, lo, hi in W_PIECES:
             load_w(g, lo, hi)
-        nc.sync.dma_start(gamma_sb[:], gamma.rearrange("(p t) o -> p (t o)", t=PACK))
 
         w2_scale = keep.tile([P, N], U8, name="w2_scale", align_bytes=64)
         w2_code = keep.tile([P, N], U32, name="w2_code", align_bytes=64)
@@ -74,8 +75,28 @@ def tile_picked_inorm_relu_e_kernel(tc, xT, w1, w2_words, w2_scales, gamma, offs
         warm_out = keep.tile([P, 1], F32, name="warm_out")
         nc.vector.memset(warm_in[:], 1.0)
         nc.scalar.activation(warm_out[:], warm_in[:], ACT.Abs_reciprocal_sqrt)
+        doubled = keep.tile([P, PACK], F32, name="doubled")
+        signs = keep.tile([P, PACK], F32, name="signs")
         neg_gamma = keep.tile([P, PACK], F32, name="neg_gamma")
         factors = keep.tile([P, PACK, 2], F32, name="factors")
+        copy_scale = keep.tile([P, 1], F32, name="copy_scale")
+        squared = keep.tile([P, PACK], F32, name="squared")
+        floored = keep.tile([P, PACK], F32, name="floored")
+        inverse = keep.tile([P, PACK], F32, name="inverse")
+        root_scale = keep.tile([P, 1], F32, name="root_scale")
+        root_bias = keep.tile([P, 2], F32, name="root_bias")
+        last_sign = signs[:, PACK - 1 : PACK]
+        nc.vector.tensor_scalar(doubled[:], gamma_sb[:], 0.0, 2.0, ALU.is_ge, ALU.mult)
+        nc.vector.tensor_scalar_add(signs[:], doubled[:], -1.0)
+        nc.vector.tensor_scalar_mul(factors[:, :, 0], gamma_sb[:], last_sign)
+        nc.vector.tensor_scalar(neg_gamma[:], gamma_sb[:], last_sign, -1.0, ALU.mult, ALU.mult)
+        nc.vector.tensor_scalar(copy_scale[:], signs[:, 0:1], last_sign, 1.0 / S, ALU.mult, ALU.mult)
+        nc.vector.tensor_mul(squared[:], gamma_sb[:], gamma_sb[:])
+        nc.vector.tensor_scalar_max(floored[:], squared[:], TINY)
+        nc.vector.reciprocal(inverse[:], floored[:])
+        nc.vector.tensor_scalar_mul(root_scale[:], inverse[:, 0:1], 1.0 / S**3)
+        nc.vector.tensor_scalar_mul(root_bias[:, 0:1], inverse[:, 0:1], EPS / S**2)
+        nc.vector.tensor_scalar_mul(root_bias[:, 1:2], inverse[:, PACK - 1 : PACK], EPS)
 
         x_code = [keep.tile([P, S], U32, name=f"x_code{g}", align_bytes=64) for g in range(PASSES)]
         x_scale = [keep.tile([P, S], U8, name=f"x_scale{g}", align_bytes=64) for g in range(PASSES)]
@@ -105,6 +126,11 @@ def tile_picked_inorm_relu_e_kernel(tc, xT, w1, w2_words, w2_scales, gamma, offs
         pieces = [(t, lo, lo + HALF) for t in range(PACK) for lo in (0, HALF)]
         banks = {}
 
+        def h_cols(t, lo, hi):
+            if (t, HALF) in banks and lo >= HALF:
+                return banks[t, HALF][:, lo - HALF : hi - HALF]
+            return banks[t, 0][:, lo:hi]
+
         dealt = [keep.tile([P, PACK, P, PACK], BF16, name=f"dealt{g}", align_bytes=64) for g in range(PASSES)]
 
         def deal(g, lo, t_lo, t_hi, on_vector):
@@ -120,44 +146,38 @@ def tile_picked_inorm_relu_e_kernel(tc, xT, w1, w2_words, w2_scales, gamma, offs
             nc.vector.quantize_mx(code[:].bitcast(FP8X4), scale[:], dealt[g][:, t].rearrange("p m j -> p (m j)"))
             for tt, lo, hi in pieces:
                 if tt == t:
+                    shared = t == 0
                     nc.tensor.matmul_mx(
-                        banks[t, lo][:],
+                        h_cols(t, lo, hi),
                         lhsT=code[:].bitcast(FP8X4),
                         lhsT_scale=scale[:],
                         rhs=x_code[g][:, lo:hi].bitcast(FP8X4),
                         rhs_scale=x_scale[g][:, lo:hi],
-                        start=(g == 0),
-                        stop=(g == PASSES - 1),
+                        start=(g == 0 and not (shared and lo > 0)),
+                        stop=(g == PASSES - 1 and not (shared and lo == 0)),
                     )
 
         for g in range(PASSES):
             for j in range(PACK):
                 gather(g, j)
             quantise_x(g)
-        spare = psum.tile([P, S], F32, name="spare", tag=f"bank{PACK - 1}_{HALF}")
+        spare = psum.tile([P, S], F32, name="spare", tag="spare")
         for lo in (0, QUARTER):
             nc.tensor.matmul_mx(
                 spare[:], lhsT=x_code[1][:, lo : lo + P].bitcast(FP8X4), lhsT_scale=x_scale[1][:, lo : lo + P],
                 rhs=x_code[0][:].bitcast(FP8X4), rhs_scale=x_scale[0][:], start=True, stop=True,
             )
-        for t, lo, hi in pieces:
+        banks[0, 0] = psum.tile([P, S], F32, name="h0_0", tag="bank0_0")
+        for t, lo, hi in pieces[2:]:
             banks[t, lo] = psum.tile([P, hi - lo], F32, name=f"h{t}_{lo}", tag=f"bank{t}_{lo}")
         for g, lo, t_lo, t_hi, on_vector in W_DEALS:
             deal(g, lo, t_lo, t_hi, on_vector)
             for t in range(t_lo, t_hi):
                 first_layer(g, t)
 
-        nc.scalar.activation(neg_gamma[:], gamma_sb[:], ACT.Copy, scale=-1.0)
-        nc.scalar.activation(factors[:, :, 0], gamma_sb[:], ACT.Copy)
-
-        def h_cols(t, lo, hi):
-            if (t, HALF) in banks and lo >= HALF:
-                return banks[t, HALF][:, lo - HALF : hi - HALF]
-            return banks[t, 0][:, lo:hi]
-
         stats = {t: keep.tile([P, 2, 6], F32, name=f"stats{t}") for t in range(1, PACK)}
         moments = [keep.tile([P, 2], F32, name=f"moments{t}") for t in range(PACK)]
-        rstd = [keep.tile([P, 1], F32, name=f"rstd{t}") for t in range(PACK)]
+        rstd = {t: keep.tile([P, 1], F32, name=f"rstd{t}") for t in (1, 2)}
         affine = [keep.tile([P, 2], F32, name=f"affine{t}") for t in range(PACK)]
         z_planes = [keep.tile([P, PACK, HALF], BF16, name=f"z_planes{u}") for u in range(2)]
 
@@ -166,21 +186,26 @@ def tile_picked_inorm_relu_e_kernel(tc, xT, w1, w2_words, w2_scales, gamma, offs
 
         h0 = keep.tile([P, S], F32, name="h0")
         squares = keep.tile([P, S], BF16, name="squares")
-        sums = keep.tile([P, 3], F32, name="sums")
-        scaled_sums = keep.tile([P, 2], F32, name="scaled_sums")
+        sums = keep.tile([P, 2], F32, name="sums")
 
         def finish_stats(t):
             nc.vector.bn_aggr(moments[t][:], stats[t][:].rearrange("p u s -> p (u s)"))
+            if t == PACK - 1:
+                nc.scalar.activation(
+                    affine[t][:, 0:1], moments[t][:, 1:2], ACT.Abs_reciprocal_sqrt,
+                    scale=inverse[:, t : t + 1], bias=root_bias[:, 1:2],
+                )
+                return
             nc.scalar.activation(rstd[t][:], moments[t][:, 1:2], ACT.Abs_reciprocal_sqrt, bias=EPS)
             nc.scalar.activation(factors[:, t, 1:2], moments[t][:, 0:1], ACT.Copy, scale=neg_gamma[:, t : t + 1])
 
         def scale_factors(t):
-            width = 1 if t == 0 else 2
-            nc.scalar.activation(affine[t][:, :width], factors[:, t, :width], ACT.Copy, scale=rstd[t][:])
+            nc.scalar.activation(affine[t][:], factors[:, t, :], ACT.Copy, scale=rstd[t][:])
 
-        def normalise_scalar(t, u):
+        def normalise_scalar(t, c):
             nc.scalar.activation(
-                z_planes[u][:, t, :], h_cols(t, u * HALF, (u + 1) * HALF), ACT.Relu,
+                z_planes[c // 2][:, t, (c % 2) * QUARTER : (c % 2 + 1) * QUARTER],
+                h_cols(t, c * QUARTER, (c + 1) * QUARTER), ACT.Identity,
                 scale=affine[t][:, 0:1], bias=affine[t][:, 1:2],
             )
 
@@ -189,36 +214,33 @@ def tile_picked_inorm_relu_e_kernel(tc, xT, w1, w2_words, w2_scales, gamma, offs
             src = h0[:, lo:hi] if t == 0 else h_cols(t, lo, hi)
             nc.vector.tensor_scalar(
                 z_planes[u][:, t, lo - u * HALF : hi - u * HALF], src,
-                moments[t][:, 0:1], affine[t][:, 0:1], ALU.add if t == 0 else ALU.subtract, ALU.mult,
+                moments[t][:, 0:1], affine[t][:, 0:1], ALU.subtract, ALU.mult,
             )
 
-        for u in range(2):
-            nc.scalar.activation(h0[:, u * HALF : (u + 1) * HALF], banks[0, u * HALF][:], ACT.Copy, accum_out=sums[:, u : u + 1])
-        nc.scalar.activation(scaled_sums[:], sums[:, 0:2], ACT.Copy, scale=-1.0 / S, accum_out=moments[0][:, 0:1])
-        nc.scalar.activation(squares[:], h0[:], ACT.Square, bias=moments[0][:, 0:1], accum_out=sums[:, 2:3])
-        nc.scalar.activation(rstd[0][:], sums[:, 2:3], ACT.Abs_reciprocal_sqrt, scale=1.0 / S, bias=EPS)
+        nc.scalar.activation(h0[:], banks[0, 0][:], ACT.Copy, scale=copy_scale[:], accum_out=sums[:, 0:1])
+        nc.scalar.activation(squares[:], h0[:], ACT.Square, scale=-float(S), bias=sums[:, 0:1], accum_out=sums[:, 1:2])
         half_stats(1, 0)
         half_stats(1, 1)
-        half_stats(2, 0)
         finish_stats(1)
-        scale_factors(0)
         scale_factors(1)
-        half_stats(2, 1)
-        half_stats(3, 0)
-        normalise_scalar(1, 0)
-        finish_stats(2)
-        normalise_scalar(1, 1)
+        nc.scalar.activation(
+            affine[0][:, 0:1], sums[:, 1:2], ACT.Abs_reciprocal_sqrt, scale=root_scale[:], bias=root_bias[:, 0:1]
+        )
+        nc.scalar.activation(moments[0][:, 0:1], sums[:, 0:1], ACT.Copy, scale=1.0 / S)
+        for t in (2, 3):
+            half_stats(t, 0)
+            half_stats(t, 1)
+            finish_stats(t)
         scale_factors(2)
-        half_stats(3, 1)
-        finish_stats(3)
+        for c in range(4):
+            normalise_scalar(1, c)
         normalise_vector(0, 0, HALF)
         normalise_vector(0, HALF, S)
-        scale_factors(3)
         normalise_vector(2, 0, HALF)
-        normalise_scalar(2, 1)
-        normalise_vector(3, 0, QUARTER)
-        normalise_vector(3, QUARTER, HALF)
-        normalise_scalar(3, 1)
+        normalise_scalar(2, 3)
+        normalise_scalar(2, 2)
+        for c in (3, 0, 1, 2):
+            normalise_vector(3, c * QUARTER, (c + 1) * QUARTER)
 
         woven = [keep.tile([P, QUARTER, PACK], BF16, name=f"woven{c}", align_bytes=64) for c in range(4)]
 
@@ -227,15 +249,15 @@ def tile_picked_inorm_relu_e_kernel(tc, xT, w1, w2_words, w2_scales, gamma, offs
             dst = woven[c][:].rearrange("p (c i) t -> p c t i", i=WALK)
             split = Z_SPLITS[c] // WALK
             if split > 0:
-                nc.vector.tensor_scalar_max(dst[:, :split], src[:, :split], 0.0)
+                nc.vector.tensor_scalar(dst[:, :split], src[:, :split], last_sign, 0.0, ALU.mult, ALU.max)
             if split < QUARTER // WALK:
-                nc.scalar.activation(dst[:, split:], src[:, split:], ACT.Relu)
+                nc.scalar.activation(dst[:, split:], src[:, split:], ACT.Relu, scale=last_sign)
 
         def second_layer(c):
             code = keep.tile([P, QUARTER], U32, name=f"z_code{c}", align_bytes=64)
             scale = keep.tile([P, QUARTER], U8, name=f"z_scale{c}", align_bytes=64)
             nc.vector.quantize_mx(code[:].bitcast(FP8X4), scale[:], woven[c][:].rearrange("p s t -> p (s t)"))
-            acc = psum.tile([P, QUARTER], F32, name=f"acc{c}", tag=f"bank{c // 2}_{(c % 2) * HALF}")
+            acc = psum.tile([P, QUARTER], F32, name=f"acc{c}", tag=("spare", "bank0_0", "bank1_0", f"bank1_{HALF}")[c])
             nc.tensor.matmul_mx(
                 acc[:], lhsT=w2_code[:].bitcast(FP8X4), lhsT_scale=w2_scale[:],
                 rhs=code[:].bitcast(FP8X4), rhs_scale=scale[:], start=True, stop=True,

@@ -24,11 +24,11 @@ PASSES = K // K_PASS
 HALF = S // 2
 QUARTER = S // 4
 W_PIECES = ((0, 0, 128), (1, 0, 128))
-W_DEALS = ((0, 0, 0, 4, 72), (1, 0, 0, 2, 80), (1, 0, 2, 4, 52))
+W_DEALS = ((0, 0, 0, 2, 128), (0, 0, 2, 4, 32), (1, 0, 0, 2, 80), (1, 0, 2, 4, 52))
 X_LOADS = ((0, 0, 2), (0, 2, 2), (1, 0, 2), (1, 2, 1), (1, 3, 1))
 WALK = 4
 Z_SPLITS = (128, 128, 40, 0)
-X_PIECES = ((0, 128, False), (128, 256, False), (256, 384, True), (384, 512, True))
+X_PIECES = ((0, 128, False), (128, 256, False), (256, 384, True), (384, 512, False))
 
 
 def tile_picked_inorm_relu_e_kernel(tc, xT, w1, w2_words, w2_scales, gamma, offs, out):
@@ -118,7 +118,7 @@ def tile_picked_inorm_relu_e_kernel(tc, xT, w1, w2_words, w2_scales, gamma, offs
                     woven[lo][:].rearrange("p (c i) j -> p c j i", i=WALK),
                     picked[g][:, lo // QUARTER].rearrange("p j (c i) -> p c j i", i=WALK),
                 )
-            for lo, hi, on_vector in X_PIECES:
+            for lo, hi, on_vector in (X_PIECES[c] for c in (0, 2, 1, 3)):
                 nc.vector.quantize_mx(
                     x_code[g][:, lo:hi].bitcast(FP8X4), x_scale[g][:, lo:hi], woven[lo][:].rearrange("p s j -> p (s j)")
                 )
@@ -138,7 +138,8 @@ def tile_picked_inorm_relu_e_kernel(tc, xT, w1, w2_words, w2_scales, gamma, offs
             dst = dealt[g][:].rearrange("p t m j -> p m j t")[:, lo : lo + src.shape[1], :, t_lo:t_hi]
             if on_vector:
                 nc.vector.tensor_copy(dst[:, :on_vector], src[:, :on_vector])
-            nc.scalar.copy(dst[:, on_vector:], src[:, on_vector:])
+            if on_vector < P:
+                nc.scalar.copy(dst[:, on_vector:], src[:, on_vector:])
 
         def first_layer(g, t):
             code = keep.tile([P, P], U32, name=f"w_code{g}{t}", align_bytes=64)
@@ -162,7 +163,7 @@ def tile_picked_inorm_relu_e_kernel(tc, xT, w1, w2_words, w2_scales, gamma, offs
                 gather(g, j)
             quantise_x(g)
         spare = psum.tile([P, S], F32, name="spare", tag="spare")
-        for lo in (0, QUARTER):
+        for lo in (0, HALF):
             nc.tensor.matmul_mx(
                 spare[:], lhsT=x_code[1][:, lo : lo + P].bitcast(FP8X4), lhsT_scale=x_scale[1][:, lo : lo + P],
                 rhs=x_code[0][:].bitcast(FP8X4), rhs_scale=x_scale[0][:], start=True, stop=True,
@@ -170,9 +171,10 @@ def tile_picked_inorm_relu_e_kernel(tc, xT, w1, w2_words, w2_scales, gamma, offs
         banks[0, 0] = psum.tile([P, S], F32, name="h0_0", tag="bank0_0")
         for t, lo, hi in pieces[2:]:
             banks[t, lo] = psum.tile([P, hi - lo], F32, name=f"h{t}_{lo}", tag=f"bank{t}_{lo}")
-        for g, lo, t_lo, t_hi, on_vector in W_DEALS:
-            deal(g, lo, t_lo, t_hi, on_vector)
-            for t in range(t_lo, t_hi):
+        for g in range(PASSES):
+            for piece in W_DEALS[2 * g : 2 * g + 2]:
+                deal(*piece)
+            for t in range(PACK):
                 first_layer(g, t)
 
         stats = {t: keep.tile([P, 2, 6], F32, name=f"stats{t}") for t in range(1, PACK)}

@@ -54,13 +54,13 @@ def tile_picked_inorm_relu_e_kernel(tc, xT, w1, w2_words, w2_scales, gamma, offs
             w_raw[g, lo] = keep.tile([P, PACK, PACK * (hi - lo)], F32, name=f"w_raw{g}_{lo}")
             nc.sync.dma_start(w_raw[g, lo][:], w_rows[g, :, :, PACK * lo : PACK * hi])
 
-        nc.scalar.dma_start(gamma_sb[:], gamma.rearrange("(p t) o -> p (t o)", t=PACK))
         load_x(*X_LOADS[0])
         nc.sync.dma_start(offsets[:], offs)
         for g, j, count in X_LOADS[1:]:
             load_x(g, j, count)
         for g, lo, hi in W_PIECES:
             load_w(g, lo, hi)
+        nc.sync.dma_start(gamma_sb[:], gamma.rearrange("(p t) o -> p (t o)", t=PACK))
 
         w2_scale = keep.tile([P, N], U8, name="w2_scale", align_bytes=64)
         w2_code = keep.tile([P, N], U32, name="w2_code", align_bytes=64)
@@ -75,28 +75,6 @@ def tile_picked_inorm_relu_e_kernel(tc, xT, w1, w2_words, w2_scales, gamma, offs
         warm_out = keep.tile([P, 1], F32, name="warm_out")
         nc.vector.memset(warm_in[:], 1.0)
         nc.scalar.activation(warm_out[:], warm_in[:], ACT.Abs_reciprocal_sqrt)
-        doubled = keep.tile([P, PACK], F32, name="doubled")
-        signs = keep.tile([P, PACK], F32, name="signs")
-        neg_gamma = keep.tile([P, PACK], F32, name="neg_gamma")
-        factors = keep.tile([P, PACK, 2], F32, name="factors")
-        copy_scale = keep.tile([P, 1], F32, name="copy_scale")
-        squared = keep.tile([P, PACK], F32, name="squared")
-        floored = keep.tile([P, PACK], F32, name="floored")
-        inverse = keep.tile([P, PACK], F32, name="inverse")
-        root_scale = keep.tile([P, 1], F32, name="root_scale")
-        root_bias = keep.tile([P, 2], F32, name="root_bias")
-        last_sign = signs[:, PACK - 1 : PACK]
-        nc.vector.tensor_scalar(doubled[:], gamma_sb[:], 0.0, 2.0, ALU.is_ge, ALU.mult)
-        nc.vector.tensor_scalar_add(signs[:], doubled[:], -1.0)
-        nc.vector.tensor_scalar_mul(factors[:, :, 0], gamma_sb[:], last_sign)
-        nc.vector.tensor_scalar(neg_gamma[:], gamma_sb[:], last_sign, -1.0, ALU.mult, ALU.mult)
-        nc.vector.tensor_scalar(copy_scale[:], signs[:, 0:1], last_sign, 1.0 / S, ALU.mult, ALU.mult)
-        nc.vector.tensor_mul(squared[:], gamma_sb[:], gamma_sb[:])
-        nc.vector.tensor_scalar_max(floored[:], squared[:], TINY)
-        nc.vector.reciprocal(inverse[:], floored[:])
-        nc.vector.tensor_scalar_mul(root_scale[:], inverse[:, 0:1], 1.0 / S**3)
-        nc.vector.tensor_scalar_mul(root_bias[:, 0:1], inverse[:, 0:1], EPS / S**2)
-        nc.vector.tensor_scalar_mul(root_bias[:, 1:2], inverse[:, PACK - 1 : PACK], EPS)
 
         x_code = [keep.tile([P, S], U32, name=f"x_code{g}", align_bytes=64) for g in range(PASSES)]
         x_scale = [keep.tile([P, S], U8, name=f"x_scale{g}", align_bytes=64) for g in range(PASSES)]
@@ -177,9 +155,25 @@ def tile_picked_inorm_relu_e_kernel(tc, xT, w1, w2_words, w2_scales, gamma, offs
             for t in range(PACK):
                 first_layer(g, t)
 
+        doubled = keep.tile([P, 1], F32, name="doubled")
+        last_sign = keep.tile([P, 1], F32, name="last_sign")
+        factors = keep.tile([P, PACK - 1, 2], F32, name="factors")
+        neg_gamma = keep.tile([P, PACK - 1], F32, name="neg_gamma")
+        floored = keep.tile([P, 1], F32, name="floored")
+        inverse = keep.tile([P, 1], F32, name="inverse")
+        root_bias = keep.tile([P, 1], F32, name="root_bias")
+        last_gamma = gamma_sb[:, PACK - 1 : PACK]
+        nc.vector.tensor_scalar(doubled[:], last_gamma, 0.0, 2.0, ALU.is_ge, ALU.mult)
+        nc.vector.tensor_scalar(floored[:], last_gamma, last_gamma, TINY, ALU.mult, ALU.add)
+        nc.vector.tensor_scalar_add(last_sign[:], doubled[:], -1.0)
+        nc.vector.reciprocal(inverse[:], floored[:])
+        nc.scalar.activation(factors[:, :, 0], gamma_sb[:, : PACK - 1], ACT.Copy, scale=last_sign[:])
+        nc.scalar.activation(neg_gamma[:], factors[:, :, 0], ACT.Copy, scale=-1.0)
+        nc.scalar.activation(root_bias[:], inverse[:], ACT.Copy, scale=EPS)
+
         stats = {t: keep.tile([P, 2, 6], F32, name=f"stats{t}") for t in range(1, PACK)}
         moments = [keep.tile([P, 2], F32, name=f"moments{t}") for t in range(PACK)]
-        rstd = {t: keep.tile([P, 1], F32, name=f"rstd{t}") for t in (1, 2)}
+        rstd = {t: keep.tile([P, 1], F32, name=f"rstd{t}") for t in range(PACK - 1)}
         affine = [keep.tile([P, 2], F32, name=f"affine{t}") for t in range(PACK)]
         z_planes = [keep.tile([P, PACK, HALF], BF16, name=f"z_planes{u}") for u in range(2)]
 
@@ -195,7 +189,7 @@ def tile_picked_inorm_relu_e_kernel(tc, xT, w1, w2_words, w2_scales, gamma, offs
             if t == PACK - 1:
                 nc.scalar.activation(
                     affine[t][:, 0:1], moments[t][:, 1:2], ACT.Abs_reciprocal_sqrt,
-                    scale=inverse[:, t : t + 1], bias=root_bias[:, 1:2],
+                    scale=inverse[:], bias=root_bias[:],
                 )
                 return
             nc.scalar.activation(rstd[t][:], moments[t][:, 1:2], ACT.Abs_reciprocal_sqrt, bias=EPS)
@@ -219,15 +213,14 @@ def tile_picked_inorm_relu_e_kernel(tc, xT, w1, w2_words, w2_scales, gamma, offs
                 moments[t][:, 0:1], affine[t][:, 0:1], ALU.subtract, ALU.mult,
             )
 
-        nc.scalar.activation(h0[:], banks[0, 0][:], ACT.Copy, scale=copy_scale[:], accum_out=sums[:, 0:1])
+        nc.scalar.activation(h0[:], banks[0, 0][:], ACT.Copy, scale=1.0 / S, accum_out=sums[:, 0:1])
         nc.scalar.activation(squares[:], h0[:], ACT.Square, scale=-float(S), bias=sums[:, 0:1], accum_out=sums[:, 1:2])
         half_stats(1, 0)
         half_stats(1, 1)
         finish_stats(1)
         scale_factors(1)
-        nc.scalar.activation(
-            affine[0][:, 0:1], sums[:, 1:2], ACT.Abs_reciprocal_sqrt, scale=root_scale[:], bias=root_bias[:, 0:1]
-        )
+        nc.scalar.activation(rstd[0][:], sums[:, 1:2], ACT.Abs_reciprocal_sqrt, scale=1.0 / S**3, bias=EPS / S**2)
+        nc.scalar.activation(affine[0][:, 0:1], factors[:, 0, 0:1], ACT.Copy, scale=rstd[0][:])
         nc.scalar.activation(moments[0][:, 0:1], sums[:, 0:1], ACT.Copy, scale=1.0 / S)
         for t in (2, 3):
             half_stats(t, 0)
@@ -251,9 +244,9 @@ def tile_picked_inorm_relu_e_kernel(tc, xT, w1, w2_words, w2_scales, gamma, offs
             dst = woven[c][:].rearrange("p (c i) t -> p c t i", i=WALK)
             split = Z_SPLITS[c] // WALK
             if split > 0:
-                nc.vector.tensor_scalar(dst[:, :split], src[:, :split], last_sign, 0.0, ALU.mult, ALU.max)
+                nc.vector.tensor_scalar(dst[:, :split], src[:, :split], last_sign[:], 0.0, ALU.mult, ALU.max)
             if split < QUARTER // WALK:
-                nc.scalar.activation(dst[:, split:], src[:, split:], ACT.Relu, scale=last_sign)
+                nc.scalar.activation(dst[:, split:], src[:, split:], ACT.Relu, scale=last_sign[:])
 
         def second_layer(c):
             code = keep.tile([P, QUARTER], U32, name=f"z_code{c}", align_bytes=64)

@@ -248,24 +248,28 @@ def tile_picked_inorm_relu_e_kernel(tc, xT, w1, w2_words, w2_scales, gamma, offs
             if split < QUARTER // WALK:
                 nc.scalar.activation(dst[:, split:], src[:, split:], ACT.Relu, scale=last_sign[:])
 
-        def second_layer(c):
-            code = keep.tile([P, QUARTER], U32, name=f"z_code{c}", align_bytes=64)
-            scale = keep.tile([P, QUARTER], U8, name=f"z_scale{c}", align_bytes=64)
-            nc.vector.quantize_mx(code[:].bitcast(FP8X4), scale[:], woven[c][:].rearrange("p s t -> p (s t)"))
-            acc = psum.tile([P, QUARTER], F32, name=f"acc{c}", tag=("spare", "bank0_0", "bank1_0", f"bank1_{HALF}")[c])
+        result = keep.tile([P, S], F32, name="result")
+
+        def second_layer(lo, hi, bank, copy):
+            code = keep.tile([P, hi - lo], U32, name=f"z_code{lo}", align_bytes=64)
+            scale = keep.tile([P, hi - lo], U8, name=f"z_scale{lo}", align_bytes=64)
+            points = woven[lo // QUARTER][:, lo % QUARTER : lo % QUARTER + hi - lo]
+            nc.vector.quantize_mx(code[:].bitcast(FP8X4), scale[:], points.rearrange("p s t -> p (s t)"))
+            acc = psum.tile([P, hi - lo], F32, name=f"acc{lo}", tag=bank)
             nc.tensor.matmul_mx(
                 acc[:], lhsT=w2_code[:].bitcast(FP8X4), lhsT_scale=w2_scale[:],
                 rhs=code[:].bitcast(FP8X4), rhs_scale=scale[:], start=True, stop=True,
             )
-            result = keep.tile([P, QUARTER], F32, name=f"result{c}")
-            (nc.vector.tensor_copy if c == 2 else nc.scalar.copy)(result[:], acc[:])
-            nc.sync.dma_start(out[:, c * QUARTER : (c + 1) * QUARTER], result[:])
+            copy(result[:, lo:hi], acc[:])
 
         weave(0)
         weave(3)
         weave(1)
-        second_layer(0)
+        second_layer(0, 128, "spare", nc.scalar.copy)
+        nc.sync.dma_start(out[:, :QUARTER], result[:, :QUARTER])
         weave(2)
-        second_layer(1)
-        second_layer(3)
-        second_layer(2)
+        second_layer(128, 256, "bank0_0", nc.scalar.copy)
+        second_layer(384, 512, "bank1_0", nc.scalar.copy)
+        second_layer(256, 320, f"bank1_{HALF}", nc.vector.tensor_copy)
+        second_layer(320, 384, "bank2_0", nc.scalar.copy)
+        nc.sync.dma_start(out[:, QUARTER:], result[:, QUARTER:])

@@ -24,11 +24,11 @@ PASSES = K // K_PASS
 HALF = S // 2
 QUARTER = S // 4
 W_PIECES = ((0, 0, 128), (1, 0, 128))
-W_DEALS = ((0, 0, 0, 2, 128), (0, 0, 2, 4, 32), (1, 0, 0, 2, 80), (1, 0, 2, 4, 52))
-X_LOADS = ((0, 0, 2), (0, 2, 2), (1, 0, 2), (1, 2, 1), (1, 3, 1))
+W_DEALS = ((0, 0, 0, 2, 80), (0, 0, 2, 4, 52), (1, 0, 0, 2, 80), (1, 0, 2, 4, 52))
+X_LOADS = ((0, 0, 4), (1, 0, 3), (1, 3, 1))
 WALK = 4
 Z_SPLITS = (128, 128, 40, 0)
-X_PIECES = ((0, 128, False), (128, 256, False), (256, 384, True), (384, 512, False))
+WARM = ((0, 256), (256, 128), (384, 64))
 
 
 def tile_picked_inorm_relu_e_kernel(tc, xT, w1, w2_words, w2_scales, gamma, offs, out):
@@ -76,30 +76,38 @@ def tile_picked_inorm_relu_e_kernel(tc, xT, w1, w2_words, w2_scales, gamma, offs
         nc.vector.memset(warm_in[:], 1.0)
         nc.scalar.activation(warm_out[:], warm_in[:], ACT.Abs_reciprocal_sqrt)
 
-        x_code = [keep.tile([P, S], U32, name=f"x_code{g}", align_bytes=64) for g in range(PASSES)]
-        x_scale = [keep.tile([P, S], U8, name=f"x_scale{g}", align_bytes=64) for g in range(PASSES)]
-        picked = [keep.tile([P, 4, PACK, QUARTER], BF16, name=f"picked{g}") for g in range(PASSES)]
+        x_code = {}
+        x_scale = {(g, u): keep.tile([P, HALF], U8, name=f"x_scale{g}{u}", align_bytes=64) for g in range(PASSES) for u in range(2)}
+        picked = [[keep.tile([P, PACK, HALF], F32, name=f"picked{g}{u}") for u in range(2)] for g in range(PASSES)]
 
-        def gather(g, j):
-            if (g, j) == (PASSES - 1, PACK - 1):
-                for q in range(4):
-                    nc.vector.tensor_copy(picked[g][:, q, j, :], planes[g, j].indirect(offsets[:, q * 8 : (q + 1) * 8]))
+        def gather(g, j, lo, hi, on_vector):
+            window = planes[g, j].indirect(offsets[:, lo // 16 : hi // 16])
+            dst = picked[g][lo // HALF][:, j, lo % HALF : lo % HALF + hi - lo]
+            if on_vector:
+                nc.vector.tensor_copy(dst, window)
             else:
-                nc.vector.tensor_copy(picked[g][:, :, j, :], planes[g, j].indirect(offsets[:]))
+                nc.scalar.activation(dst, window, ACT.Copy)
 
-        def quantise_x(g):
-            woven = {}
-            for lo, hi, on_vector in X_PIECES:
-                woven[lo] = keep.tile([P, hi - lo, PACK], BF16, name=f"x_woven{g}_{lo}", align_bytes=64)
-                copy = nc.vector.tensor_copy if on_vector else nc.scalar.copy
+        x_woven = {}
+
+        def weave_x(g):
+            for c in (0, 3, 1, 2):
+                x_woven[g, c] = keep.tile([P, QUARTER, PACK], BF16, name=f"x_woven{g}_{c}", align_bytes=64)
+                copy = nc.vector.tensor_copy if c < 2 else nc.scalar.copy
                 copy(
-                    woven[lo][:].rearrange("p (c i) j -> p c j i", i=WALK),
-                    picked[g][:, lo // QUARTER].rearrange("p j (c i) -> p c j i", i=WALK),
+                    x_woven[g, c][:].rearrange("p (c i) j -> p c j i", i=WALK),
+                    picked[g][c // 2][:, :, (c % 2) * QUARTER : (c % 2 + 1) * QUARTER].rearrange("p j (c i) -> p c j i", i=WALK),
                 )
-            for lo, hi, on_vector in (X_PIECES[c] for c in (0, 2, 1, 3)):
-                nc.vector.quantize_mx(
-                    x_code[g][:, lo:hi].bitcast(FP8X4), x_scale[g][:, lo:hi], woven[lo][:].rearrange("p s j -> p (s j)")
-                )
+
+        def quantise_x(g, c):
+            u = c // 2
+            if (g, u) not in x_code:
+                tag = "dealt00" if (g, u) == (1, 1) else f"x_code{g}{u}"
+                x_code[g, u] = keep.tile([P, HALF], U32, name=f"x_code{g}{u}", tag=tag, align_bytes=64)
+            cols = slice((c % 2) * QUARTER, (c % 2 + 1) * QUARTER)
+            nc.vector.quantize_mx(
+                x_code[g, u][:, cols].bitcast(FP8X4), x_scale[g, u][:, cols], x_woven[g, c][:].rearrange("p s j -> p (s j)")
+            )
 
         pieces = [(t, lo, lo + HALF) for t in range(PACK) for lo in (0, HALF)]
         banks = {}
@@ -109,11 +117,13 @@ def tile_picked_inorm_relu_e_kernel(tc, xT, w1, w2_words, w2_scales, gamma, offs
                 return banks[t, HALF][:, lo - HALF : hi - HALF]
             return banks[t, 0][:, lo:hi]
 
-        dealt = [keep.tile([P, PACK, P, PACK], BF16, name=f"dealt{g}", align_bytes=64) for g in range(PASSES)]
+        dealt = {}
 
         def deal(g, lo, t_lo, t_hi, on_vector):
             src = w_raw[g, lo][:].rearrange("p j (m t) -> p m j t", t=PACK)[:, :, :, t_lo:t_hi]
-            dst = dealt[g][:].rearrange("p t m j -> p m j t")[:, lo : lo + src.shape[1], :, t_lo:t_hi]
+            pair = t_lo // 2
+            dealt[g, pair] = keep.tile([P, 2, P, PACK], BF16, name=f"dealt{g}{pair}", tag=f"dealt{g}{pair}", align_bytes=64)
+            dst = dealt[g, pair][:].rearrange("p t m j -> p m j t")
             if on_vector:
                 nc.vector.tensor_copy(dst[:, :on_vector], src[:, :on_vector])
             if on_vector < P:
@@ -122,7 +132,7 @@ def tile_picked_inorm_relu_e_kernel(tc, xT, w1, w2_words, w2_scales, gamma, offs
         def first_layer(g, t):
             code = keep.tile([P, P], U32, name=f"w_code{g}{t}", align_bytes=64)
             scale = keep.tile([P, P], U8, name=f"w_scale{g}{t}", align_bytes=64)
-            nc.vector.quantize_mx(code[:].bitcast(FP8X4), scale[:], dealt[g][:, t].rearrange("p m j -> p (m j)"))
+            nc.vector.quantize_mx(code[:].bitcast(FP8X4), scale[:], dealt[g, t // 2][:, t % 2].rearrange("p m j -> p (m j)"))
             for tt, lo, hi in pieces:
                 if tt == t:
                     shared = t == 0
@@ -130,30 +140,46 @@ def tile_picked_inorm_relu_e_kernel(tc, xT, w1, w2_words, w2_scales, gamma, offs
                         h_cols(t, lo, hi),
                         lhsT=code[:].bitcast(FP8X4),
                         lhsT_scale=scale[:],
-                        rhs=x_code[g][:, lo:hi].bitcast(FP8X4),
-                        rhs_scale=x_scale[g][:, lo:hi],
+                        rhs=x_code[g, lo // HALF][:].bitcast(FP8X4),
+                        rhs_scale=x_scale[g, lo // HALF][:],
                         start=(g == 0 and not (shared and lo > 0)),
                         stop=(g == PASSES - 1 and not (shared and lo == 0)),
                     )
 
         for g in range(PASSES):
             for j in range(PACK):
-                gather(g, j)
-            quantise_x(g)
+                if (g, j) == (PASSES - 1, PACK - 1):
+                    gather(g, j, HALF, 3 * QUARTER, True)
+                    gather(g, j, 3 * QUARTER, S, False)
+                else:
+                    gather(g, j, HALF, S, False)
+                gather(g, j, 0, HALF, True)
+            weave_x(g)
+            for c in range(4 if g == 0 else 1):
+                quantise_x(g, c)
         spare = psum.tile([P, S], F32, name="spare", tag="spare")
-        for lo in (0, HALF):
+        for lo, width in WARM:
             nc.tensor.matmul_mx(
-                spare[:], lhsT=x_code[1][:, lo : lo + P].bitcast(FP8X4), lhsT_scale=x_scale[1][:, lo : lo + P],
-                rhs=x_code[0][:].bitcast(FP8X4), rhs_scale=x_scale[0][:], start=True, stop=True,
+                spare[:, lo : lo + width],
+                lhsT=x_code[1, 0][:, :QUARTER].bitcast(FP8X4), lhsT_scale=x_scale[1, 0][:, :QUARTER],
+                rhs=x_code[0, 0][:, :width].bitcast(FP8X4), rhs_scale=x_scale[0, 0][:, :width], start=True, stop=True,
             )
         banks[0, 0] = psum.tile([P, S], F32, name="h0_0", tag="bank0_0")
         for t, lo, hi in pieces[2:]:
             banks[t, lo] = psum.tile([P, hi - lo], F32, name=f"h{t}_{lo}", tag=f"bank{t}_{lo}")
-        for g in range(PASSES):
-            for piece in W_DEALS[2 * g : 2 * g + 2]:
-                deal(*piece)
-            for t in range(PACK):
-                first_layer(g, t)
+        deal(*W_DEALS[0])
+        quantise_x(1, 1)
+        first_layer(0, 0)
+        first_layer(0, 1)
+        deal(*W_DEALS[1])
+        quantise_x(1, 3)
+        first_layer(0, 2)
+        first_layer(0, 3)
+        quantise_x(1, 2)
+        deal(*W_DEALS[2])
+        deal(*W_DEALS[3])
+        for t in range(PACK):
+            first_layer(1, t)
 
         doubled = keep.tile([P, 1], F32, name="doubled")
         last_sign = keep.tile([P, 1], F32, name="last_sign")

@@ -24,7 +24,7 @@ PASSES = K // K_PASS
 HALF = S // 2
 QUARTER = S // 4
 W_PIECES = ((0, 0, 128), (1, 0, 128))
-W_DEALS = ((0, 0, 0, 2, 80), (0, 0, 2, 4, 52), (1, 0, 0, 2, 80), (1, 0, 2, 4, 52))
+W_DEALS = ((0, 0, 0, 2, 96), (0, 0, 2, 4, 64), (1, 0, 0, 2, 80), (1, 0, 2, 4, 52))
 X_LOADS = ((0, 0, 4), (1, 0, 3), (1, 3, 1))
 WALK = 4
 Z_SPLITS = (128, 128, 40, 0)
@@ -91,9 +91,9 @@ def tile_picked_inorm_relu_e_kernel(tc, xT, w1, w2_words, w2_scales, gamma, offs
         x_woven = {}
 
         def weave_x(g):
-            for c in (0, 3, 1, 2):
+            for c in range(4):
                 x_woven[g, c] = keep.tile([P, QUARTER, PACK], BF16, name=f"x_woven{g}_{c}", align_bytes=64)
-                copy = nc.vector.tensor_copy if c < 2 else nc.scalar.copy
+                copy = nc.vector.tensor_copy if c < 3 else nc.scalar.copy
                 copy(
                     x_woven[g, c][:].rearrange("p (c i) j -> p c j i", i=WALK),
                     picked[g][c // 2][:, :, (c % 2) * QUARTER : (c % 2 + 1) * QUARTER].rearrange("p j (c i) -> p c j i", i=WALK),
@@ -149,11 +149,11 @@ def tile_picked_inorm_relu_e_kernel(tc, xT, w1, w2_words, w2_scales, gamma, offs
         for g in range(PASSES):
             for j in range(PACK):
                 if (g, j) == (PASSES - 1, PACK - 1):
-                    gather(g, j, HALF, 3 * QUARTER, True)
-                    gather(g, j, 3 * QUARTER, S, False)
+                    for c in range(4):
+                        gather(g, j, c * QUARTER, (c + 1) * QUARTER, False)
                 else:
                     gather(g, j, HALF, S, False)
-                gather(g, j, 0, HALF, True)
+                    gather(g, j, 0, HALF, True)
             weave_x(g)
             for c in range(4 if g == 0 else 1):
                 quantise_x(g, c)
@@ -172,10 +172,10 @@ def tile_picked_inorm_relu_e_kernel(tc, xT, w1, w2_words, w2_scales, gamma, offs
         first_layer(0, 0)
         first_layer(0, 1)
         deal(*W_DEALS[1])
-        quantise_x(1, 3)
+        quantise_x(1, 2)
         first_layer(0, 2)
         first_layer(0, 3)
-        quantise_x(1, 2)
+        quantise_x(1, 3)
         deal(*W_DEALS[2])
         deal(*W_DEALS[3])
         for t in range(PACK):

@@ -24,8 +24,8 @@ PASSES = K // K_PASS
 HALF = S // 2
 QUARTER = S // 4
 W_PIECES = ((0, 0, 128), (1, 0, 128))
-W_DEALS = ((0, 0, 0, 2, 96), (0, 0, 2, 4, 64), (1, 0, 0, 2, 80), (1, 0, 2, 4, 52))
-X_LOADS = ((0, 0, 4), (1, 0, 3), (1, 3, 1))
+W_DEALS = ((0, 0, 0, 2, 88), (0, 0, 2, 4, 64), (1, 0, 0, 2, 80), (1, 0, 2, 4, 52))
+X_LOADS = ((0, 0, 2), (0, 2, 2), (1, 0, 1), (1, 1, 2), (1, 3, 1))
 WALK = 4
 Z_SPLITS = (128, 128, 40, 0)
 WARM = ((0, 256), (256, 128), (384, 64))
@@ -46,7 +46,8 @@ def tile_picked_inorm_relu_e_kernel(tc, xT, w1, w2_words, w2_scales, gamma, offs
 
         def load_x(g, j, count):
             rows = keep.tile([P, count, T], F32, name=f"rows{g}{j}")
-            nc.sync.dma_start(rows[:], x_rows[g, :, j : j + count])
+            queue = nc.scalar if (g, j) in ((0, 2), (1, 0)) else nc.sync
+            queue.dma_start(rows[:], x_rows[g, :, j : j + count])
             for i in range(count):
                 planes[g, j + i] = rows[:, i, :]
 
@@ -55,8 +56,9 @@ def tile_picked_inorm_relu_e_kernel(tc, xT, w1, w2_words, w2_scales, gamma, offs
             nc.sync.dma_start(w_raw[g, lo][:], w_rows[g, :, :, PACK * lo : PACK * hi])
 
         load_x(*X_LOADS[0])
+        load_x(*X_LOADS[1])
         nc.sync.dma_start(offsets[:], offs)
-        for g, j, count in X_LOADS[1:]:
+        for g, j, count in X_LOADS[2:]:
             load_x(g, j, count)
         for g, lo, hi in W_PIECES:
             load_w(g, lo, hi)

@@ -28,7 +28,6 @@ W_DEALS = ((0, 0, 0, 2, 88), (0, 0, 2, 4, 64), (1, 0, 0, 2, 80), (1, 0, 2, 4, 52
 X_LOADS = ((0, 0, 2), (0, 2, 2), (1, 0, 1), (1, 1, 2), (1, 3, 1))
 WALK = 4
 Z_SPLITS = (128, 128, 40, 0)
-WARM = ((0, 256), (256, 128), (384, 64))
 
 
 def tile_picked_inorm_relu_e_kernel(tc, xT, w1, w2_words, w2_scales, gamma, offs, out):
@@ -159,13 +158,6 @@ def tile_picked_inorm_relu_e_kernel(tc, xT, w1, w2_words, w2_scales, gamma, offs
             weave_x(g)
             for c in range(4 if g == 0 else 1):
                 quantise_x(g, c)
-        spare = psum.tile([P, S], F32, name="spare", tag="spare")
-        for lo, width in WARM:
-            nc.tensor.matmul_mx(
-                spare[:, lo : lo + width],
-                lhsT=x_code[1, 0][:, :QUARTER].bitcast(FP8X4), lhsT_scale=x_scale[1, 0][:, :QUARTER],
-                rhs=x_code[0, 0][:, :width].bitcast(FP8X4), rhs_scale=x_scale[0, 0][:, :width], start=True, stop=True,
-            )
         banks[0, 0] = psum.tile([P, S], F32, name="h0_0", tag="bank0_0")
         for t, lo, hi in pieces[2:]:
             banks[t, lo] = psum.tile([P, hi - lo], F32, name=f"h{t}_{lo}", tag=f"bank{t}_{lo}")

@@ -27,6 +27,7 @@ W_PIECES = ((0, 0, 128), (1, 0, 128))
 W_DEALS = ((0, 0, 0, 2, 88), (0, 0, 2, 4, 64), (1, 0, 0, 2, 80), (1, 0, 2, 4, 52))
 X_LOADS = ((0, 0, 2), (0, 2, 2), (1, 0, 1), (1, 1, 2), (1, 3, 1))
 WALK = 4
+WARM_PASSES, WARM_ROWS = 2, 32
 Z_SPLITS = (128, 128, 40, 0)
 
 
@@ -77,8 +78,10 @@ def tile_picked_inorm_relu_e_kernel(tc, xT, w1, w2_words, w2_scales, gamma, offs
         nc.vector.memset(warm_in[:], 1.0)
         nc.scalar.activation(warm_out[:], warm_in[:], ACT.Abs_reciprocal_sqrt)
 
-        x_code = {}
-        x_scale = {(g, u): keep.tile([P, HALF], U8, name=f"x_scale{g}{u}", align_bytes=64) for g in range(PASSES) for u in range(2)}
+        first_code = keep.tile([P, S], U32, name="first_code", align_bytes=64)
+        first_scale = keep.tile([P, S], U8, name="first_scale", align_bytes=64)
+        x_code = {(0, u): first_code[:, u * HALF : (u + 1) * HALF] for u in range(2)}
+        x_scale = {(0, u): first_scale[:, u * HALF : (u + 1) * HALF] for u in range(2)}
         picked = [[keep.tile([P, PACK, HALF], F32, name=f"picked{g}{u}") for u in range(2)] for g in range(PASSES)]
 
         def gather(g, j, lo, hi, on_vector):
@@ -103,8 +106,9 @@ def tile_picked_inorm_relu_e_kernel(tc, xT, w1, w2_words, w2_scales, gamma, offs
         def quantise_x(g, c):
             u = c // 2
             if (g, u) not in x_code:
-                tag = "dealt00" if (g, u) == (1, 1) else f"x_code{g}{u}"
-                x_code[g, u] = keep.tile([P, HALF], U32, name=f"x_code{g}{u}", tag=tag, align_bytes=64)
+                tag = "dealt00" if u == 1 else f"x_code{g}{u}"
+                x_code[g, u] = keep.tile([P, HALF], U32, name=f"x_code{g}{u}", tag=tag, align_bytes=64)[:]
+                x_scale[g, u] = keep.tile([P, HALF], U8, name=f"x_scale{g}{u}", align_bytes=64)[:]
             cols = slice((c % 2) * QUARTER, (c % 2 + 1) * QUARTER)
             nc.vector.quantize_mx(
                 x_code[g, u][:, cols].bitcast(FP8X4), x_scale[g, u][:, cols], x_woven[g, c][:].rearrange("p s j -> p (s j)")
@@ -141,8 +145,8 @@ def tile_picked_inorm_relu_e_kernel(tc, xT, w1, w2_words, w2_scales, gamma, offs
                         h_cols(t, lo, hi),
                         lhsT=code[:].bitcast(FP8X4),
                         lhsT_scale=scale[:],
-                        rhs=x_code[g, lo // HALF][:].bitcast(FP8X4),
-                        rhs_scale=x_scale[g, lo // HALF][:],
+                        rhs=x_code[g, lo // HALF].bitcast(FP8X4),
+                        rhs_scale=x_scale[g, lo // HALF],
                         start=(g == 0 and not (shared and lo > 0)),
                         stop=(g == PASSES - 1 and not (shared and lo == 0)),
                     )
@@ -158,6 +162,13 @@ def tile_picked_inorm_relu_e_kernel(tc, xT, w1, w2_words, w2_scales, gamma, offs
             weave_x(g)
             for c in range(4 if g == 0 else 1):
                 quantise_x(g, c)
+        spare = psum.tile([P, S], F32, name="spare", tag="spare")
+        for turn in range(WARM_PASSES):
+            nc.tensor.matmul_mx(
+                spare[:WARM_ROWS, :],
+                lhsT=x_code[1, 0][:, :WARM_ROWS].bitcast(FP8X4), lhsT_scale=x_scale[1, 0][:, :WARM_ROWS],
+                rhs=first_code[:].bitcast(FP8X4), rhs_scale=first_scale[:], start=True, stop=True,
+            )
         banks[0, 0] = psum.tile([P, S], F32, name="h0_0", tag="bank0_0")
         for t, lo, hi in pieces[2:]:
             banks[t, lo] = psum.tile([P, hi - lo], F32, name=f"h{t}_{lo}", tag=f"bank{t}_{lo}")

@@ -27,7 +27,7 @@ W_PIECES = ((0, 0, 128), (1, 0, 128))
 W_DEALS = ((0, 0, 0, 2, 88), (0, 0, 2, 4, 64), (1, 0, 0, 2, 80), (1, 0, 2, 4, 52))
 X_LOADS = ((0, 0, 2), (0, 2, 2), (1, 0, 1), (1, 1, 2), (1, 3, 1))
 WALK = 4
-WARM_PASSES, WARM_ROWS = 2, 32
+WARM_ROWS = 32
 Z_SPLITS = (128, 128, 40, 0)
 
 
@@ -162,13 +162,6 @@ def tile_picked_inorm_relu_e_kernel(tc, xT, w1, w2_words, w2_scales, gamma, offs
             weave_x(g)
             for c in range(4 if g == 0 else 1):
                 quantise_x(g, c)
-        spare = psum.tile([P, S], F32, name="spare", tag="spare")
-        for turn in range(WARM_PASSES):
-            nc.tensor.matmul_mx(
-                spare[:WARM_ROWS, :],
-                lhsT=x_code[1, 0][:, :WARM_ROWS].bitcast(FP8X4), lhsT_scale=x_scale[1, 0][:, :WARM_ROWS],
-                rhs=first_code[:].bitcast(FP8X4), rhs_scale=first_scale[:], start=True, stop=True,
-            )
         banks[0, 0] = psum.tile([P, S], F32, name="h0_0", tag="bank0_0")
         for t, lo, hi in pieces[2:]:
             banks[t, lo] = psum.tile([P, hi - lo], F32, name=f"h{t}_{lo}", tag=f"bank{t}_{lo}")
@@ -267,6 +260,14 @@ def tile_picked_inorm_relu_e_kernel(tc, xT, w1, w2_words, w2_scales, gamma, offs
         normalise_scalar(2, 2)
         for c in (3, 0, 1, 2):
             normalise_vector(3, c * QUARTER, (c + 1) * QUARTER)
+
+        for bank in ("bank1_0", "bank2_0", "bank3_0"):
+            idle = psum.tile([P, S], F32, name=f"idle_{bank}", tag=bank)
+            nc.tensor.matmul_mx(
+                idle[:WARM_ROWS, :],
+                lhsT=x_code[1, 0][:, :WARM_ROWS].bitcast(FP8X4), lhsT_scale=x_scale[1, 0][:, :WARM_ROWS],
+                rhs=first_code[:].bitcast(FP8X4), rhs_scale=first_scale[:], start=True, stop=True,
+            )
 
         woven = [keep.tile([P, QUARTER, PACK], BF16, name=f"woven{c}", align_bytes=64) for c in range(4)]
 

@@ -167,6 +167,13 @@ def tile_picked_inorm_relu_e_kernel(tc, xT, w1, w2_words, w2_scales, gamma, offs
             banks[t, lo] = psum.tile([P, hi - lo], F32, name=f"h{t}_{lo}", tag=f"bank{t}_{lo}")
         deal(*W_DEALS[0])
         quantise_x(1, 1)
+        spare = psum.tile([P, S], F32, name="spare", tag="spare")
+        for width in (S, QUARTER):
+            nc.tensor.matmul_mx(
+                spare[:WARM_ROWS, :width],
+                lhsT=x_code[1, 0][:, QUARTER : QUARTER + WARM_ROWS].bitcast(FP8X4), lhsT_scale=x_scale[1, 0][:, QUARTER : QUARTER + WARM_ROWS],
+                rhs=first_code[:, :width].bitcast(FP8X4), rhs_scale=first_scale[:, :width], start=True, stop=True,
+            )
         first_layer(0, 0)
         first_layer(0, 1)
         deal(*W_DEALS[1])
@@ -261,7 +268,7 @@ def tile_picked_inorm_relu_e_kernel(tc, xT, w1, w2_words, w2_scales, gamma, offs
         for c in (3, 0, 1, 2):
             normalise_vector(3, c * QUARTER, (c + 1) * QUARTER)
 
-        for bank in ("bank1_0", "bank2_0", "bank3_0"):
+        for bank in ("bank1_0", f"bank1_{HALF}"):
             idle = psum.tile([P, S], F32, name=f"idle_{bank}", tag=bank)
             nc.tensor.matmul_mx(
                 idle[:WARM_ROWS, :],

@@ -27,7 +27,6 @@ W_PIECES = ((0, 0, 128), (1, 0, 128))
 W_DEALS = ((0, 0, 0, 2, 88), (0, 0, 2, 4, 64), (1, 0, 0, 2, 80), (1, 0, 2, 4, 52))
 X_LOADS = ((0, 0, 2), (0, 2, 2), (1, 0, 1), (1, 1, 2), (1, 3, 1))
 WALK = 4
-WARM_ROWS = 32
 Z_SPLITS = (128, 128, 40, 0)
 
 
@@ -167,13 +166,6 @@ def tile_picked_inorm_relu_e_kernel(tc, xT, w1, w2_words, w2_scales, gamma, offs
             banks[t, lo] = psum.tile([P, hi - lo], F32, name=f"h{t}_{lo}", tag=f"bank{t}_{lo}")
         deal(*W_DEALS[0])
         quantise_x(1, 1)
-        spare = psum.tile([P, S], F32, name="spare", tag="spare")
-        for width in (S, QUARTER):
-            nc.tensor.matmul_mx(
-                spare[:WARM_ROWS, :width],
-                lhsT=x_code[1, 0][:, QUARTER : QUARTER + WARM_ROWS].bitcast(FP8X4), lhsT_scale=x_scale[1, 0][:, QUARTER : QUARTER + WARM_ROWS],
-                rhs=first_code[:, :width].bitcast(FP8X4), rhs_scale=first_scale[:, :width], start=True, stop=True,
-            )
         first_layer(0, 0)
         first_layer(0, 1)
         deal(*W_DEALS[1])
@@ -267,14 +259,6 @@ def tile_picked_inorm_relu_e_kernel(tc, xT, w1, w2_words, w2_scales, gamma, offs
         normalise_scalar(2, 2)
         for c in (3, 0, 1, 2):
             normalise_vector(3, c * QUARTER, (c + 1) * QUARTER)
-
-        for bank in ("bank1_0", f"bank1_{HALF}"):
-            idle = psum.tile([P, S], F32, name=f"idle_{bank}", tag=bank)
-            nc.tensor.matmul_mx(
-                idle[:WARM_ROWS, :],
-                lhsT=x_code[1, 0][:, :WARM_ROWS].bitcast(FP8X4), lhsT_scale=x_scale[1, 0][:, :WARM_ROWS],
-                rhs=first_code[:].bitcast(FP8X4), rhs_scale=first_scale[:], start=True, stop=True,
-            )
 
         woven = [keep.tile([P, QUARTER, PACK], BF16, name=f"woven{c}", align_bytes=64) for c in range(4)]
 

from contextlib import ExitStack

import concourse.mybir as mybir

K, T, S, H, N = 1024, 2048, 512, 512, 128
FLOPS = 2 * K * H * S + 2 * H * N * S
EPS = 1e-5
TINY = 2.0**-100

F32 = mybir.dt.float32
BF16 = mybir.dt.bfloat16
I32 = mybir.dt.int32
U32 = mybir.dt.uint32
U16 = mybir.dt.uint16
U8 = mybir.dt.uint8
FP8X4 = mybir.dt.float8_e4m3fn_x4
ALU = mybir.AluOpType
ACT = mybir.ActivationFunctionType

P = 128
PACK = 4
K_PASS = P * PACK
PASSES = K // K_PASS
HALF = S // 2
QUARTER = S // 4
W_PIECES = ((0, 0, 128), (1, 0, 128))
W_DEALS = ((0, 0, 0, 2, 88), (0, 0, 2, 4, 64), (1, 0, 0, 2, 80), (1, 0, 2, 4, 52))
X_LOADS = ((0, 0, 2), (0, 2, 2), (1, 0, 1), (1, 1, 2), (1, 3, 1))
WALK = 4
Z_SPLITS = (128, 128, 40, 0)


def tile_picked_inorm_relu_e_kernel(tc, xT, w1, w2_words, w2_scales, gamma, offs, out):
    nc = tc.nc
    with ExitStack() as ctx:
        keep = ctx.enter_context(tc.tile_pool(name="keep", bufs=1))
        psum = ctx.enter_context(tc.psum_pool(name="psum", bufs=1))

        offsets = keep.tile([P, S // 16], U16, name="offsets")
        gamma_sb = keep.tile([P, PACK], F32, name="gamma_sb")
        x_rows = xT.rearrange("(g p j) c -> g p j c", p=P, j=PACK)
        w_rows = w1.rearrange("(g p j) c -> g p j c", p=P, j=PACK)
        planes = {}
        w_raw = {}

        def load_x(g, j, count):
            rows = keep.tile([P, count, T], F32, name=f"rows{g}{j}")
            queue = nc.scalar if (g, j) in ((0, 2), (1, 0)) else nc.sync
            queue.dma_start(rows[:], x_rows[g, :, j : j + count])
            for i in range(count):
                planes[g, j + i] = rows[:, i, :]

        def load_w(g, lo, hi):
            w_raw[g, lo] = keep.tile([P, PACK, PACK * (hi - lo)], F32, name=f"w_raw{g}_{lo}")
            nc.sync.dma_start(w_raw[g, lo][:], w_rows[g, :, :, PACK * lo : PACK * hi])

        load_x(*X_LOADS[0])
        load_x(*X_LOADS[1])
        nc.sync.dma_start(offsets[:], offs)
        for g, j, count in X_LOADS[2:]:
            load_x(g, j, count)
        for g, lo, hi in W_PIECES:
            load_w(g, lo, hi)
        nc.sync.dma_start(gamma_sb[:], gamma.rearrange("(p t) o -> p (t o)", t=PACK))

        w2_scale = keep.tile([P, N], U8, name="w2_scale", align_bytes=64)
        w2_code = keep.tile([P, N], U32, name="w2_code", align_bytes=64)
        nc.vector.memset(w2_scale[:].bitcast(I32), 0)
        nc.sync.dma_start(w2_code[:].bitcast(I32), w2_words[0].rearrange("p n t -> p (n t)").bitcast(I32))
        for q in range(4):
            nc.sync.dma_start(
                w2_scale[32 * q : 32 * q + 4, :].bitcast(I32), w2_scales[0, 4 * q : 4 * q + 4, :].bitcast(I32)
            )

        warm_in = keep.tile([P, 1], F32, name="warm_in")
        warm_out = keep.tile([P, 1], F32, name="warm_out")
        nc.vector.memset(warm_in[:], 1.0)
        nc.scalar.activation(warm_out[:], warm_in[:], ACT.Abs_reciprocal_sqrt)

        first_code = keep.tile([P, S], U32, name="first_code", align_bytes=64)
        first_scale = keep.tile([P, S], U8, name="first_scale", align_bytes=64)
        x_code = {(0, u): first_code[:, u * HALF : (u + 1) * HALF] for u in range(2)}
        x_scale = {(0, u): first_scale[:, u * HALF : (u + 1) * HALF] for u in range(2)}
        picked = [[keep.tile([P, PACK, HALF], F32, name=f"picked{g}{u}") for u in range(2)] for g in range(PASSES)]

        def gather(g, j, lo, hi, on_vector):
            window = planes[g, j].indirect(offsets[:, lo // 16 : hi // 16])
            dst = picked[g][lo // HALF][:, j, lo % HALF : lo % HALF + hi - lo]
            if on_vector:
                nc.vector.tensor_copy(dst, window)
            else:
                nc.scalar.activation(dst, window, ACT.Copy)

        x_woven = {}

        def weave_x(g):
            for c in range(4):
                x_woven[g, c] = keep.tile([P, QUARTER, PACK], BF16, name=f"x_woven{g}_{c}", align_bytes=64)
                copy = nc.vector.tensor_copy if c < 3 else nc.scalar.copy
                copy(
                    x_woven[g, c][:].rearrange("p (c i) j -> p c j i", i=WALK),
                    picked[g][c // 2][:, :, (c % 2) * QUARTER : (c % 2 + 1) * QUARTER].rearrange("p j (c i) -> p c j i", i=WALK),
                )

        def quantise_x(g, c):
            u = c // 2
            if (g, u) not in x_code:
                tag = "dealt00" if u == 1 else f"x_code{g}{u}"
                x_code[g, u] = keep.tile([P, HALF], U32, name=f"x_code{g}{u}", tag=tag, align_bytes=64)[:]
                x_scale[g, u] = keep.tile([P, HALF], U8, name=f"x_scale{g}{u}", align_bytes=64)[:]
            cols = slice((c % 2) * QUARTER, (c % 2 + 1) * QUARTER)
            nc.vector.quantize_mx(
                x_code[g, u][:, cols].bitcast(FP8X4), x_scale[g, u][:, cols], x_woven[g, c][:].rearrange("p s j -> p (s j)")
            )

        pieces = [(t, lo, lo + HALF) for t in range(PACK) for lo in (0, HALF)]
        banks = {}

        def h_cols(t, lo, hi):
            if (t, HALF) in banks and lo >= HALF:
                return banks[t, HALF][:, lo - HALF : hi - HALF]
            return banks[t, 0][:, lo:hi]

        dealt = {}

        def deal(g, lo, t_lo, t_hi, on_vector):
            src = w_raw[g, lo][:].rearrange("p j (m t) -> p m j t", t=PACK)[:, :, :, t_lo:t_hi]
            pair = t_lo // 2
            dealt[g, pair] = keep.tile([P, 2, P, PACK], BF16, name=f"dealt{g}{pair}", tag=f"dealt{g}{pair}", align_bytes=64)
            dst = dealt[g, pair][:].rearrange("p t m j -> p m j t")
            if on_vector:
                nc.vector.tensor_copy(dst[:, :on_vector], src[:, :on_vector])
            if on_vector < P:
                nc.scalar.copy(dst[:, on_vector:], src[:, on_vector:])

        def first_layer(g, t):
            code = keep.tile([P, P], U32, name=f"w_code{g}{t}", align_bytes=64)
            scale = keep.tile([P, P], U8, name=f"w_scale{g}{t}", align_bytes=64)
            nc.vector.quantize_mx(code[:].bitcast(FP8X4), scale[:], dealt[g, t // 2][:, t % 2].rearrange("p m j -> p (m j)"))
            for tt, lo, hi in pieces:
                if tt == t:
                    shared = t == 0
                    nc.tensor.matmul_mx(
                        h_cols(t, lo, hi),
                        lhsT=code[:].bitcast(FP8X4),
                        lhsT_scale=scale[:],
                        rhs=x_code[g, lo // HALF].bitcast(FP8X4),
                        rhs_scale=x_scale[g, lo // HALF],
                        start=(g == 0 and not (shared and lo > 0)),
                        stop=(g == PASSES - 1 and not (shared and lo == 0)),
                    )

        for g in range(PASSES):
            for j in range(PACK):
                if (g, j) == (PASSES - 1, PACK - 1):
                    for c in range(4):
                        gather(g, j, c * QUARTER, (c + 1) * QUARTER, False)
                else:
                    gather(g, j, HALF, S, False)
                    gather(g, j, 0, HALF, True)
            weave_x(g)
            for c in range(4 if g == 0 else 1):
                quantise_x(g, c)
        banks[0, 0] = psum.tile([P, S], F32, name="h0_0", tag="bank0_0")
        for t, lo, hi in pieces[2:]:
            banks[t, lo] = psum.tile([P, hi - lo], F32, name=f"h{t}_{lo}", tag=f"bank{t}_{lo}")
        deal(*W_DEALS[0])
        quantise_x(1, 1)
        first_layer(0, 0)
        first_layer(0, 1)
        deal(*W_DEALS[1])
        quantise_x(1, 2)
        first_layer(0, 2)
        first_layer(0, 3)
        quantise_x(1, 3)
        deal(*W_DEALS[2])
        deal(*W_DEALS[3])
        for t in range(PACK):
            first_layer(1, t)

        doubled = keep.tile([P, 1], F32, name="doubled")
        last_sign = keep.tile([P, 1], F32, name="last_sign")
        factors = keep.tile([P, PACK - 1, 2], F32, name="factors")
        neg_gamma = keep.tile([P, PACK - 1], F32, name="neg_gamma")
        floored = keep.tile([P, 1], F32, name="floored")
        inverse = keep.tile([P, 1], F32, name="inverse")
        root_bias = keep.tile([P, 1], F32, name="root_bias")
        last_gamma = gamma_sb[:, PACK - 1 : PACK]
        nc.vector.tensor_scalar(doubled[:], last_gamma, 0.0, 2.0, ALU.is_ge, ALU.mult)
        nc.vector.tensor_scalar(floored[:], last_gamma, last_gamma, TINY, ALU.mult, ALU.add)
        nc.vector.tensor_scalar_add(last_sign[:], doubled[:], -1.0)
        nc.vector.reciprocal(inverse[:], floored[:])
        nc.scalar.activation(factors[:, :, 0], gamma_sb[:, : PACK - 1], ACT.Copy, scale=last_sign[:])
        nc.scalar.activation(neg_gamma[:], factors[:, :, 0], ACT.Copy, scale=-1.0)
        nc.scalar.activation(root_bias[:], inverse[:], ACT.Copy, scale=EPS)

        stats = {t: keep.tile([P, 2, 6], F32, name=f"stats{t}") for t in range(1, PACK)}
        moments = [keep.tile([P, 2], F32, name=f"moments{t}") for t in range(PACK)]
        rstd = {t: keep.tile([P, 1], F32, name=f"rstd{t}") for t in range(PACK - 1)}
        affine = [keep.tile([P, 2], F32, name=f"affine{t}") for t in range(PACK)]
        z_planes = [keep.tile([P, PACK, HALF], BF16, name=f"z_planes{u}") for u in range(2)]

        def half_stats(t, u):
            nc.vector.bn_stats(stats[t][:, u, :], h_cols(t, u * HALF, (u + 1) * HALF))

        h0 = keep.tile([P, S], F32, name="h0")
        squares = keep.tile([P, S], BF16, name="squares")
        sums = keep.tile([P, 2], F32, name="sums")

        def finish_stats(t):
            nc.vector.bn_aggr(moments[t][:], stats[t][:].rearrange("p u s -> p (u s)"))
            if t == PACK - 1:
                nc.scalar.activation(
                    affine[t][:, 0:1], moments[t][:, 1:2], ACT.Abs_reciprocal_sqrt,
                    scale=inverse[:], bias=root_bias[:],
                )
                return
            nc.scalar.activation(rstd[t][:], moments[t][:, 1:2], ACT.Abs_reciprocal_sqrt, bias=EPS)
            nc.scalar.activation(factors[:, t, 1:2], moments[t][:, 0:1], ACT.Copy, scale=neg_gamma[:, t : t + 1])

        def scale_factors(t):
            nc.scalar.activation(affine[t][:], factors[:, t, :], ACT.Copy, scale=rstd[t][:])

        def normalise_scalar(t, c):
            nc.scalar.activation(
                z_planes[c // 2][:, t, (c % 2) * QUARTER : (c % 2 + 1) * QUARTER],
                h_cols(t, c * QUARTER, (c + 1) * QUARTER), ACT.Identity,
                scale=affine[t][:, 0:1], bias=affine[t][:, 1:2],
            )

        def normalise_vector(t, lo, hi):
            u = lo // HALF
            src = h0[:, lo:hi] if t == 0 else h_cols(t, lo, hi)
            nc.vector.tensor_scalar(
                z_planes[u][:, t, lo - u * HALF : hi - u * HALF], src,
                moments[t][:, 0:1], affine[t][:, 0:1], ALU.subtract, ALU.mult,
            )

        nc.scalar.activation(h0[:], banks[0, 0][:], ACT.Copy, scale=1.0 / S, accum_out=sums[:, 0:1])
        nc.scalar.activation(squares[:], h0[:], ACT.Square, scale=-float(S), bias=sums[:, 0:1], accum_out=sums[:, 1:2])
        half_stats(1, 0)
        half_stats(1, 1)
        finish_stats(1)
        scale_factors(1)
        nc.scalar.activation(rstd[0][:], sums[:, 1:2], ACT.Abs_reciprocal_sqrt, scale=1.0 / S**3, bias=EPS / S**2)
        nc.scalar.activation(affine[0][:, 0:1], factors[:, 0, 0:1], ACT.Copy, scale=rstd[0][:])
        nc.scalar.activation(moments[0][:, 0:1], sums[:, 0:1], ACT.Copy, scale=1.0 / S)
        for t in (2, 3):
            half_stats(t, 0)
            half_stats(t, 1)
            finish_stats(t)
        scale_factors(2)
        for c in range(4):
            normalise_scalar(1, c)
        normalise_vector(0, 0, HALF)
        normalise_vector(0, HALF, S)
        normalise_vector(2, 0, HALF)
        normalise_scalar(2, 3)
        normalise_scalar(2, 2)
        for c in (3, 0, 1, 2):
            normalise_vector(3, c * QUARTER, (c + 1) * QUARTER)

        woven = [keep.tile([P, QUARTER, PACK], BF16, name=f"woven{c}", align_bytes=64) for c in range(4)]

        def weave(c):
            src = z_planes[c // 2][:, :, (c % 2) * QUARTER : (c % 2 + 1) * QUARTER].rearrange("p t (c i) -> p c t i", i=WALK)
            dst = woven[c][:].rearrange("p (c i) t -> p c t i", i=WALK)
            split = Z_SPLITS[c] // WALK
            if split > 0:
                nc.vector.tensor_scalar(dst[:, :split], src[:, :split], last_sign[:], 0.0, ALU.mult, ALU.max)
            if split < QUARTER // WALK:
                nc.scalar.activation(dst[:, split:], src[:, split:], ACT.Relu, scale=last_sign[:])

        result = keep.tile([P, S], F32, name="result")

        def second_layer(lo, hi, bank, copy):
            code = keep.tile([P, hi - lo], U32, name=f"z_code{lo}", align_bytes=64)
            scale = keep.tile([P, hi - lo], U8, name=f"z_scale{lo}", align_bytes=64)
            points = woven[lo // QUARTER][:, lo % QUARTER : lo % QUARTER + hi - lo]
            nc.vector.quantize_mx(code[:].bitcast(FP8X4), scale[:], points.rearrange("p s t -> p (s t)"))
            acc = psum.tile([P, hi - lo], F32, name=f"acc{lo}", tag=bank)
            nc.tensor.matmul_mx(
                acc[:], lhsT=w2_code[:].bitcast(FP8X4), lhsT_scale=w2_scale[:],
                rhs=code[:].bitcast(FP8X4), rhs_scale=scale[:], start=True, stop=True,
            )
            copy(result[:, lo:hi], acc[:])

        weave(0)
        weave(3)
        weave(1)
        second_layer(0, 128, "spare", nc.scalar.copy)
        nc.sync.dma_start(out[:, :QUARTER], result[:, :QUARTER])
        weave(2)
        second_layer(128, 256, "bank0_0", nc.scalar.copy)
        second_layer(384, 512, "bank1_0", nc.scalar.copy)
        second_layer(256, 320, f"bank1_{HALF}", nc.vector.tensor_copy)
        second_layer(320, 384, "bank2_0", nc.scalar.copy)
        nc.sync.dma_start(out[:, QUARTER:], result[:, QUARTER:])
